import numpy as np
import ml_dtypes


def mxq(x, axis, fmt="e4m3"):
    dtype, down = {"e4m3": (ml_dtypes.float8_e4m3fn, 7), "e5m2": (ml_dtypes.float8_e5m2, 14)}[fmt]
    v = np.moveaxis(np.asarray(x, np.float32).astype(ml_dtypes.bfloat16).astype(np.float64), axis, -1)
    blocks = v.reshape(v.shape[:-1] + (-1, 32))
    amax = np.abs(blocks).max(-1, keepdims=True)
    byte = np.maximum(np.where(amax > 0, np.frexp(amax)[1] - 1 + 127, 0) - down, 1)
    scale = np.exp2(byte - 127.0)
    codes = (blocks / scale).astype(np.float32).astype(dtype).astype(np.float64)
    return np.moveaxis((codes * scale).reshape(v.shape), -1, axis)


WIDE = False


def mx_kscale(k):
    if not WIDE:
        return np.ones(k)
    levels = np.array([10, -10, 5, -5, 0])
    if k % 512:
        return np.exp2(np.random.permutation(np.resize(levels, k // 32))).repeat(32)
    a = np.empty((k // 512, 16))
    for p in range(k // 512):
        a[p, :8] = np.random.permutation(np.resize(levels, 8))
        for g in range(8):
            far = levels[np.abs(levels - a[p, g]) >= 10]
            a[p, g + 8] = far[np.random.randint(len(far))]
    return np.exp2(a.ravel()).repeat(32)


def f64(x):
    return np.asarray(x).astype(np.float64)


def striped(idx):
    return np.tile(np.asarray(idx).reshape(-1, 16).T, (8, 1)).astype(np.uint16)


def unstriped(offs):
    return offs[:16].T.reshape(-1).astype(np.int64)


E2M1 = np.array([0.0, 0.5, 1.0, 1.5, 2.0, 3.0, 4.0, 6.0, -0.0, -0.5, -1.0, -1.5, -2.0, -3.0, -4.0, -6.0])


def pack_weight(w, fmt):
    k, n = w.shape
    w = f64(np.asarray(w, np.float32).astype(ml_dtypes.bfloat16)).reshape(k // 32, 32, n)
    amax = np.abs(w).max(1)
    if fmt == "e4m3":
        byte = np.frexp(amax)[1] - 1 + 127 - 7
    else:
        mant, ex = np.frexp(amax / 6.0)
        byte = np.where(mant > 0.5, ex, ex - 1) + 127
    byte = np.clip(np.where(amax > 0, byte, 1), 1, 254)
    scaled = (w * np.exp2(127.0 - byte)[:, None, :]).reshape(k, n).astype(np.float32)
    by_word = np.ascontiguousarray(scaled.reshape(k // 512, 128, 4, n).transpose(0, 1, 3, 2))
    if fmt == "e4m3":
        words = by_word.astype(ml_dtypes.float8_e4m3fn).view(np.uint8)
    else:
        c = by_word.astype(ml_dtypes.float4_e2m1fn).view(np.uint8) & 0xF
        words = (c[..., 0::2] | (c[..., 1::2] << 4)).reshape(k // 512, 128, 2 * n)
    return np.ascontiguousarray(words), np.ascontiguousarray(byte.astype(np.uint8).reshape(k // 512, 16, n))


def unpack_weight(words, scales, fmt):
    g, _, n = scales.shape
    words = np.ascontiguousarray(words).reshape(g, 128, n, -1)
    if fmt == "e4m3":
        vals = words.view(ml_dtypes.float8_e4m3fn).astype(np.float64)
    else:
        nib = np.empty((g, 128, n, 4), np.uint8)
        nib[..., 0::2] = words & 0xF
        nib[..., 1::2] = words >> 4
        vals = E2M1[nib]
    vals = vals * np.repeat(np.exp2(scales.astype(np.float64) - 127.0), 8, axis=1)[..., None]
    return vals.transpose(0, 1, 3, 2).reshape(g * 512, n)


B, N, T, D, DV, NQ = 1, 512, 2048, 1024, 128, 128
CAP = 2.0


def setup_inputs():
    n = np.random.standard_normal
    idx = np.sort(np.random.permutation(T)[:B * N].reshape(B, N), axis=1).reshape(-1)
    s = mx_kscale(D)[:, None]
    u = np.ones(T)
    u[idx] = mx_kscale(B * N)
    r = np.random.uniform(0.5, 2.0, T)
    qp = [pack_weight(x, "e4m3") for x in n((B, D, NQ)) * s * (0.80 / np.sqrt(D))]
    k = n((D, T)) / s
    v = n((DV, T)) / (u * r)
    kp = pack_weight(k, "e2m1")
    return {
        "q_words": np.stack([x[0] for x in qp]),
        "q_scales": np.stack([x[1] for x in qp]),
        "k_words": np.ascontiguousarray(kp[0].reshape(D // 1024, 2, 128, T, 2).transpose(0, 2, 3, 1, 4)).reshape(D // 1024, 128, T, 4),
        "k_scales": kp[1],
        "vT": v.astype(np.float32),
        "vs": np.tile(u * r, (128, 1)).astype(np.float32),
        "offs": striped(idx),
    }


def reference(q_words, q_scales, k_words, k_scales, vT, vs, offs):
    idx = unstriped(offs)
    k = unpack_weight(k_words.reshape(D // 1024, 128, T, 2, 2).transpose(0, 3, 1, 2, 4).reshape(D // 512, 128, 2 * T), k_scales, "e2m1")
    v = f64(vT)
    pick = lambda x: x[:, idx].reshape(x.shape[0], B, N).transpose(1, 0, 2)
    q = np.stack([unpack_weight(q_words[b], q_scales[b], "e4m3") for b in range(B)])
    score = q.transpose(0, 2, 1) @ pick(k)
    score = CAP * np.tanh(score / CAP)
    p = np.square(np.maximum(score, 0.0))
    total = p.sum(-1, keepdims=True) + 1.0
    w = p * pick(f64(vs))[:, :1, :]
    y = mxq(w, 2, "e4m3") @ mxq(pick(v).transpose(0, 2, 1), 1, "e4m3")
    y = y / total
    return y

@@ -1,0 +1,154 @@
+import concourse.mybir as mybir
+from concourse.masks import make_identity
+
+P = 128
+T = 2048
+N = 512
+PASSES = 2
+PACK = 4
+RUN = 8
+CAP = 2.0
+VS_ROW = 16
+
+FLOPS = 2 * 128 * 512 * 1024 + 2 * 128 * 512 * 128
+BYTES = 2 * 128 * 2048 * 4 + 2 * 16 * 2048 + 2048 * 4 + 2 * 128 * 128 * 4 + 2 * 16 * 128 + 128 * 32 * 2 + 128 * 128 * 4
+
+F32 = mybir.dt.float32
+BF16 = mybir.dt.bfloat16
+I32 = mybir.dt.int32
+U32 = mybir.dt.uint32
+U16 = mybir.dt.uint16
+U8 = mybir.dt.uint8
+FP8X4 = mybir.dt.float8_e4m3fn_x4
+FP4X4 = mybir.dt.float4_e2m1fn_x4
+ACT = mybir.ActivationFunctionType
+ALU = mybir.AluOpType
+
+
+def by_place(rows):
+    return rows.rearrange("p (j u r e) -> p u e j r", u=2, r=RUN, e=2)
+
+
+def places(tile):
+    return tile.rearrange("p (u e j r) -> p u e j r", u=2, e=2, r=RUN)
+
+
+def tile_attend_rel2_cap_srtq128n512t2048_kernel(tc, q_words, q_scales, k_words, k_scales, vT, vs, offs, out):
+    nc = tc.nc
+    with (
+        tc.tile_pool(name="sb", bufs=1) as sb,
+        tc.psum_pool(name="ps", bufs=1) as ps,
+    ):
+        offsets = sb.tile([P, N // 16], U16, name="offsets")
+        ks_pool = sb.tile([P, T], U8, name="ks_pool", align_bytes=64)
+        kw_pool = sb.tile([P, T], I32, name="kw_pool", align_bytes=64)
+        v_pool = sb.tile([P, T], F32, name="v_pool", align_bytes=64)
+        vs_pool = sb.tile([P, T], F32, name="vs_pool", tag="reused", align_bytes=64)
+        q_codes = sb.tile([P, PASSES, P], I32, name="q_codes", align_bytes=64)
+        staged = sb.tile([P, N + P], U8, name="staged", align_bytes=64)
+        planes = sb.tile([P, PASSES, N + P], U8, name="planes", align_bytes=64)
+        ident = sb.tile([P, P], F32, name="ident", align_bytes=64)
+
+        nc.vector.memset(vs_pool[:], 0.0)
+        nc.vector.memset(ks_pool[32:64, :].bitcast(I32), 0)
+        nc.vector.memset(ks_pool[64:128, :].bitcast(I32), 0)
+        nc.vector.memset(planes[:].bitcast(I32), 0)
+        nc.vector.memset(ident[:], 0.0)
+        make_identity(nc, ident[:], nomemset=True)
+
+        nc.sync.dma_start(offsets[:], offs)
+        nc.sync.dma_start(ks_pool[0:32, :].bitcast(I32), k_scales.rearrange("o f t -> f o t").bitcast(I32))
+        nc.sync.dma_start(kw_pool[:], k_words[0].rearrange("g t b -> g (t b)").bitcast(I32))
+        nc.sync.dma_start(q_codes[:], q_words[0].rearrange("o g q r -> g o (q r)").bitcast(I32))
+        nc.sync.dma_start(v_pool[:], vT)
+        nc.scalar.dma_start(staged[0:32, N:].bitcast(I32), q_scales[0].rearrange("o f q -> f o q").bitcast(I32))
+        nc.scalar.dma_start(vs_pool[VS_ROW : VS_ROW + 1, :], vs[0:1, :])
+        warm = sb.tile([P, 1], F32, name="warm")
+        nc.scalar.activation(warm[32:64, :], vs_pool[32:64, 0:1], ACT.Tanh)
+
+        ks_rows = sb.tile([P, N], U8, name="ks_rows", align_bytes=64)
+        nc.vector.tensor_copy(ks_rows[:], ks_pool[:].indirect(offsets[:]))
+        nc.vector.tensor_copy(places(staged[:, 0:N]), by_place(ks_rows[:]))
+        for quad in range(4):
+            nc.scalar.dma_start(
+                planes[32 * quad : 32 * quad + 4, :, :].bitcast(I32),
+                staged[8 * quad : 8 * quad + 8, :].bitcast(I32),
+            )
+
+        vs_rows = sb.tile([P, N], F32, name="vs_rows", align_bytes=64)
+        nc.vector.tensor_copy(vs_rows[:], vs_pool[:].indirect(offsets[:]))
+        vs_placed = sb.tile([P, N], F32, name="vs_placed", align_bytes=64)
+        nc.scalar.copy(places(vs_placed[:]), by_place(vs_rows[:]))
+        vs_ps = ps.tile([P, PACK, P], F32, name="vs_ps")
+        for t in range(PACK):
+            nc.tensor.transpose(vs_ps[:, t, :], vs_placed[:, t * P : (t + 1) * P], ident[:])
+        vs_slot = sb.tile([P, 1, PACK], F32, name="vs_slot")
+        nc.scalar.copy(vs_slot[:, 0, :], vs_ps[:, :, VS_ROW])
+
+        k_pairs = sb.tile([P, N], U32, name="k_pairs", tag="reused", align_bytes=64)
+        nc.vector.tensor_copy(k_pairs[:], kw_pool[:].bitcast(U32).indirect(offsets[:]))
+        halves = k_pairs[:].bitcast(U16).rearrange("p (j u r e o) -> p u e o j r", u=2, r=RUN, e=2, o=PASSES)
+        th = sb.tile([P, PACK, P], F32, name="th", align_bytes=64)
+        for t in range(PACK):
+            k_codes = sb.tile([P, PASSES, 2 * P], U8, name=f"k_codes{t}", align_bytes=64)
+            nc.vector.tensor_copy(k_codes[:].bitcast(U16).rearrange("p o (j r) -> p o j r", r=RUN), halves[:, t // 2, t % 2])
+            score = ps.tile([P, P], F32, name=f"score{t}", tag=f"bank{t}")
+            for o in range(PASSES):
+                nc.tensor.matmul_mx(
+                    out=score[:],
+                    lhsT=k_codes[:, o, :].bitcast(FP4X4),
+                    lhsT_scale=planes[:, o, t * P : (t + 1) * P],
+                    rhs=q_codes[:, o, :].bitcast(FP8X4),
+                    rhs_scale=planes[:, o, N:],
+                    start=(o == 0),
+                    stop=(o == PASSES - 1),
+                )
+            nc.scalar.activation(th[:, t, :], score[:], ACT.Tanh, scale=1.0 / CAP)
+
+        v_rows = sb.tile([P, 2, N // 2], BF16, name="v_rows", align_bytes=64)
+        nc.vector.tensor_copy(v_rows[:].rearrange("p u (j s) -> p j u s", s=2 * RUN), v_pool[:].indirect(offsets[:]))
+        v_ps = ps.tile([P, 2, P], F32, name="v_ps", tag=f"bank{PACK - 1}")
+        for u in range(2):
+            nc.tensor.transpose(v_ps[:, u, :], v_rows[:, u, :].bitcast(F32), ident[:])
+        v_bf = sb.tile([P, P * PACK], BF16, name="v_bf", align_bytes=64)
+        nc.scalar.copy(v_bf[:].bitcast(F32).rearrange("p (f u) -> p f u", u=2), v_ps[:].rearrange("p u f -> p f u"))
+
+        sq = sb.tile([P, PACK, P], F32, name="sq", align_bytes=64)
+        th_flat = th[:].rearrange("p t q -> p (t q)")
+        nc.vector.scalar_tensor_tensor(
+            sq[:].rearrange("p t q -> p (t q)"), th_flat, 0.0, th_flat, ALU.max, ALU.mult
+        )
+        w_bf = sb.tile([P, P, PACK], BF16, name="w_bf", align_bytes=64)
+        nc.vector.scalar_tensor_tensor(
+            w_bf[:], sq[:].rearrange("p t q -> p q t"), CAP * CAP, vs_slot[:].to_broadcast([P, P, PACK]), ALU.mult, ALU.mult
+        )
+
+        l_ps = ps.tile([P, P], F32, name="l_ps")
+        for t in range(PACK):
+            nc.tensor.matmul(l_ps[:], lhsT=sq[:, t, :], rhs=ident[:], is_transpose=True, start=(t == 0), stop=(t == PACK - 1))
+        l_terms = sb.tile([P, P], F32, name="l_terms")
+        total = sb.tile([P, 1], F32, name="total")
+        nc.scalar.activation(l_terms[:], l_ps[:], ACT.Copy, scale=CAP * CAP, bias=1.0 / P, accum_out=total[:])
+
+        w_codes = sb.tile([P, P], U32, name="w_codes", align_bytes=64)
+        w_plane = sb.tile([P, P], U8, name="w_plane", align_bytes=64)
+        v_codes = sb.tile([P, P], U32, name="v_codes", align_bytes=64)
+        v_plane = sb.tile([P, P], U8, name="v_plane", align_bytes=64)
+        nc.vector.quantize_mx(out=v_codes[:].bitcast(FP8X4), scales=v_plane[:], in_=v_bf[:])
+        nc.vector.quantize_mx(out=w_codes[:].bitcast(FP8X4), scales=w_plane[:], in_=w_bf[:].rearrange("p q t -> p (q t)"))
+        inv = sb.tile([P, 1], F32, name="inv")
+        nc.vector.reciprocal(inv[:], total[:])
+
+        y_ps = ps.tile([P, P], F32, name="y_ps")
+        nc.tensor.matmul_mx(
+            out=y_ps[:],
+            lhsT=w_codes[:].bitcast(FP8X4),
+            lhsT_scale=w_plane[:],
+            rhs=v_codes[:].bitcast(FP8X4),
+            rhs_scale=v_plane[:],
+            start=True,
+            stop=True,
+        )
+        y = sb.tile([P, P], F32, name="y")
+        nc.vector.tensor_scalar(y[:], y_ps[:], inv[:], None, ALU.mult)
+        nc.sync.dma_start(out[0], y[:])

@@ -9,6 +9,7 @@ PACK = 4
 RUN = 8
 CAP = 2.0
 VS_ROW = 16
+ROW = 1024
 
 FLOPS = 2 * 128 * 512 * 1024 + 2 * 128 * 512 * 128
 BYTES = 2 * 128 * 2048 * 4 + 2 * 16 * 2048 + 2048 * 4 + 2 * 128 * 128 * 4 + 2 * 16 * 128 + 128 * 32 * 2 + 128 * 128 * 4
@@ -45,23 +46,24 @@ def tile_attend_rel2_cap_srtq128n512t2048_kernel(tc, q_words, q_scales, k_words,
         v_pool = sb.tile([P, T], F32, name="v_pool", align_bytes=64)
         vs_pool = sb.tile([P, T], F32, name="vs_pool", tag="reused", align_bytes=64)
         q_codes = sb.tile([P, PASSES, P], I32, name="q_codes", align_bytes=64)
-        staged = sb.tile([P, N + P], U8, name="staged", align_bytes=64)
-        planes = sb.tile([P, PASSES, N + P], U8, name="planes", align_bytes=64)
+        staged = sb.tile([P, ROW], U8, name="staged", align_bytes=64)
+        planes = sb.tile([P, PASSES, ROW], U8, name="planes", align_bytes=64)
         ident = sb.tile([P, P], F32, name="ident", align_bytes=64)
 
-        nc.vector.memset(vs_pool[:], 0.0)
+        nc.vector.memset(vs_pool[:].bitcast(I32), 0)
         nc.vector.memset(ks_pool[32:64, :].bitcast(I32), 0)
         nc.vector.memset(ks_pool[64:128, :].bitcast(I32), 0)
-        nc.vector.memset(planes[:].bitcast(I32), 0)
+        nc.vector.memset(staged[:, N + P :].bitcast(I32), 0)
+        nc.vector.memset(planes[:, :, 0 : N + P].bitcast(I32), 0)
         nc.vector.memset(ident[:], 0.0)
         make_identity(nc, ident[:], nomemset=True)
 
         nc.sync.dma_start(offsets[:], offs)
-        nc.sync.dma_start(ks_pool[0:32, :].bitcast(I32), k_scales.rearrange("o f t -> f o t").bitcast(I32))
+        nc.scalar.dma_start(ks_pool[0:32, :].bitcast(I32), k_scales.rearrange("o f t -> f o t").bitcast(I32))
+        nc.scalar.dma_start(staged[0:32, N : N + P].bitcast(I32), q_scales[0].rearrange("o f q -> f o q").bitcast(I32))
         nc.sync.dma_start(kw_pool[:], k_words[0].rearrange("g t b -> g (t b)").bitcast(I32))
         nc.sync.dma_start(q_codes[:], q_words[0].rearrange("o g q r -> g o (q r)").bitcast(I32))
-        nc.sync.dma_start(v_pool[:], vT)
-        nc.scalar.dma_start(staged[0:32, N:].bitcast(I32), q_scales[0].rearrange("o f q -> f o q").bitcast(I32))
+        nc.sync.dma_start(v_pool[:], vT, max_dma_last_dim=4096)
         nc.scalar.dma_start(vs_pool[VS_ROW : VS_ROW + 1, :], vs[0:1, :])
         warm = sb.tile([P, 1], F32, name="warm")
         nc.scalar.activation(warm[32:64, :], vs_pool[32:64, 0:1], ACT.Tanh)
@@ -99,7 +101,7 @@ def tile_attend_rel2_cap_srtq128n512t2048_kernel(tc, q_words, q_scales, k_words,
                     lhsT=k_codes[:, o, :].bitcast(FP4X4),
                     lhsT_scale=planes[:, o, t * P : (t + 1) * P],
                     rhs=q_codes[:, o, :].bitcast(FP8X4),
-                    rhs_scale=planes[:, o, N:],
+                    rhs_scale=planes[:, o, N : N + P],
                     start=(o == 0),
                     stop=(o == PASSES - 1),
                 )

@@ -8,8 +8,11 @@ PASSES = 2
 PACK = 4
 RUN = 8
 CAP = 2.0
-VS_ROW = 16
+VS_ROW = 127
+KS_ROW = 96
+V_FIRST = 1280
 ROW = 1024
+WARM = 20
 
 FLOPS = 2 * 128 * 512 * 1024 + 2 * 128 * 512 * 128
 BYTES = 2 * 128 * 2048 * 4 + 2 * 16 * 2048 + 2048 * 4 + 2 * 128 * 128 * 4 + 2 * 16 * 128 + 128 * 32 * 2 + 128 * 128 * 4
@@ -43,39 +46,43 @@ def tile_attend_rel2_cap_srtq128n512t2048_kernel(tc, q_words, q_scales, k_words,
         offsets = sb.tile([P, N // 16], U16, name="offsets")
         ks_pool = sb.tile([P, T], U8, name="ks_pool", align_bytes=64)
         kw_pool = sb.tile([P, T], I32, name="kw_pool", align_bytes=64)
-        v_pool = sb.tile([P, T], F32, name="v_pool", align_bytes=64)
+        v_pool = sb.tile([P, T], F32, name="v_pool", tag="values", align_bytes=64)
         vs_pool = sb.tile([P, T], F32, name="vs_pool", tag="reused", align_bytes=64)
         q_codes = sb.tile([P, PASSES, P], I32, name="q_codes", align_bytes=64)
         staged = sb.tile([P, ROW], U8, name="staged", align_bytes=64)
         planes = sb.tile([P, PASSES, ROW], U8, name="planes", align_bytes=64)
         ident = sb.tile([P, P], F32, name="ident", align_bytes=64)
 
-        nc.vector.memset(vs_pool[:].bitcast(I32), 0)
-        nc.vector.memset(ks_pool[32:64, :].bitcast(I32), 0)
-        nc.vector.memset(ks_pool[64:128, :].bitcast(I32), 0)
-        nc.vector.memset(staged[:, N + P :].bitcast(I32), 0)
-        nc.vector.memset(planes[:, :, 0 : N + P].bitcast(I32), 0)
-        nc.vector.memset(ident[:], 0.0)
-        make_identity(nc, ident[:], nomemset=True)
+        warm = sb.tile([P, 2], F32, name="warm")
+        nc.vector.memset(vs_pool[0:VS_ROW, :].bitcast(I32), 0)
+        nc.gpsimd.memset(warm[:, 0:1], 0.0)
+        nc.gpsimd.memset(ks_pool[0:KS_ROW, :].bitcast(I32), 0)
+        nc.gpsimd.memset(staged[:, N + P :].bitcast(I32), 0)
+        nc.gpsimd.memset(planes[:, :, 0 : N + P].bitcast(I32), 0)
+        make_identity(nc, ident[:])
+        warm_ps = ps.tile([P, P], F32, name="warm_ps")
+        for i in range(WARM):
+            nc.tensor.matmul(warm_ps[:], lhsT=ident[:], rhs=ident[:], is_transpose=True, start=(i == 0), stop=(i == WARM - 1))
 
         nc.sync.dma_start(offsets[:], offs)
-        nc.scalar.dma_start(ks_pool[0:32, :].bitcast(I32), k_scales.rearrange("o f t -> f o t").bitcast(I32))
-        nc.scalar.dma_start(staged[0:32, N : N + P].bitcast(I32), q_scales[0].rearrange("o f q -> f o q").bitcast(I32))
+        nc.scalar.dma_start(ks_pool[KS_ROW:, :].bitcast(I32), k_scales.rearrange("o f t -> f o t").bitcast(I32))
+        nc.sync.dma_start(vs_pool[VS_ROW:, :], vs[0:1, :])
+        nc.scalar.dma_start(staged[KS_ROW:, N : N + P].bitcast(I32), q_scales[0].rearrange("o f q -> f o q").bitcast(I32))
         nc.sync.dma_start(kw_pool[:], k_words[0].rearrange("g t b -> g (t b)").bitcast(I32))
         nc.sync.dma_start(q_codes[:], q_words[0].rearrange("o g q r -> g o (q r)").bitcast(I32))
-        nc.sync.dma_start(v_pool[:], vT, max_dma_last_dim=4096)
-        nc.scalar.dma_start(vs_pool[VS_ROW : VS_ROW + 1, :], vs[0:1, :])
-        warm = sb.tile([P, 1], F32, name="warm")
-        nc.scalar.activation(warm[32:64, :], vs_pool[32:64, 0:1], ACT.Tanh)
+        nc.sync.dma_start(v_pool[:, 0:V_FIRST], vT[:, 0:V_FIRST])
+        nc.scalar.activation(warm[:, 1:2], warm[:, 0:1], ACT.Tanh)
 
         ks_rows = sb.tile([P, N], U8, name="ks_rows", align_bytes=64)
         nc.vector.tensor_copy(ks_rows[:], ks_pool[:].indirect(offsets[:]))
         nc.vector.tensor_copy(places(staged[:, 0:N]), by_place(ks_rows[:]))
         for quad in range(4):
-            nc.scalar.dma_start(
+            queue = nc.scalar if quad < 2 else nc.sync
+            queue.dma_start(
                 planes[32 * quad : 32 * quad + 4, :, :].bitcast(I32),
-                staged[8 * quad : 8 * quad + 8, :].bitcast(I32),
+                staged[KS_ROW + 8 * quad : KS_ROW + 8 * quad + 8, :].bitcast(I32),
             )
+        nc.sync.dma_start(v_pool[:, V_FIRST:], vT[:, V_FIRST:])
 
         vs_rows = sb.tile([P, N], F32, name="vs_rows", align_bytes=64)
         nc.vector.tensor_copy(vs_rows[:], vs_pool[:].indirect(offsets[:]))
@@ -115,12 +122,11 @@ def tile_attend_rel2_cap_srtq128n512t2048_kernel(tc, q_words, q_scales, k_words,
         v_bf = sb.tile([P, P * PACK], BF16, name="v_bf", align_bytes=64)
         nc.scalar.copy(v_bf[:].bitcast(F32).rearrange("p (f u) -> p f u", u=2), v_ps[:].rearrange("p u f -> p f u"))
 
-        sq = sb.tile([P, PACK, P], F32, name="sq", align_bytes=64)
-        th_flat = th[:].rearrange("p t q -> p (t q)")
-        nc.vector.scalar_tensor_tensor(
-            sq[:].rearrange("p t q -> p (t q)"), th_flat, 0.0, th_flat, ALU.max, ALU.mult
-        )
-        w_bf = sb.tile([P, P, PACK], BF16, name="w_bf", align_bytes=64)
+        sq = sb.tile([P, PACK, P], F32, name="sq", tag="values", align_bytes=64)
+        for u in range(2):
+            half = th[:, 2 * u : 2 * u + 2, :]
+            nc.vector.scalar_tensor_tensor(sq[:, 2 * u : 2 * u + 2, :], half, 0.0, half, ALU.max, ALU.mult)
+        w_bf = sb.tile([P, P, PACK], BF16, name="w_bf", tag="weights", align_bytes=64)
         nc.vector.scalar_tensor_tensor(
             w_bf[:], sq[:].rearrange("p t q -> p q t"), CAP * CAP, vs_slot[:].to_broadcast([P, P, PACK]), ALU.mult, ALU.mult
         )
@@ -138,7 +144,7 @@ def tile_attend_rel2_cap_srtq128n512t2048_kernel(tc, q_words, q_scales, k_words,
         v_plane = sb.tile([P, P], U8, name="v_plane", align_bytes=64)
         nc.vector.quantize_mx(out=v_codes[:].bitcast(FP8X4), scales=v_plane[:], in_=v_bf[:])
         nc.vector.quantize_mx(out=w_codes[:].bitcast(FP8X4), scales=w_plane[:], in_=w_bf[:].rearrange("p q t -> p (q t)"))
-        inv = sb.tile([P, 1], F32, name="inv")
+        inv = sb.tile([P, 1], F32, name="inv", tag="weights", align_bytes=64)
         nc.vector.reciprocal(inv[:], total[:])
 
         y_ps = ps.tile([P, P], F32, name="y_ps")

@@ -10,7 +10,7 @@ RUN = 8
 CAP = 2.0
 VS_ROW = 127
 KS_ROW = 96
-V_FIRST = 1280
+V_FIRST = 1024
 ROW = 1024
 WARM = 20
 
@@ -123,9 +123,9 @@ def tile_attend_rel2_cap_srtq128n512t2048_kernel(tc, q_words, q_scales, k_words,
         nc.scalar.copy(v_bf[:].bitcast(F32).rearrange("p (f u) -> p f u", u=2), v_ps[:].rearrange("p u f -> p f u"))
 
         sq = sb.tile([P, PACK, P], F32, name="sq", tag="values", align_bytes=64)
-        for u in range(2):
-            half = th[:, 2 * u : 2 * u + 2, :]
-            nc.vector.scalar_tensor_tensor(sq[:, 2 * u : 2 * u + 2, :], half, 0.0, half, ALU.max, ALU.mult)
+        for first, last in ((0, 2), (2, 3), (3, 4)):
+            part = th[:, first:last, :]
+            nc.vector.scalar_tensor_tensor(sq[:, first:last, :], part, 0.0, part, ALU.max, ALU.mult)
         w_bf = sb.tile([P, P, PACK], BF16, name="w_bf", tag="weights", align_bytes=64)
         nc.vector.scalar_tensor_tensor(
             w_bf[:], sq[:].rearrange("p t q -> p q t"), CAP * CAP, vs_slot[:].to_broadcast([P, P, PACK]), ALU.mult, ALU.mult

@@ -10,9 +10,8 @@ RUN = 8
 CAP = 2.0
 VS_ROW = 127
 KS_ROW = 96
-V_FIRST = 1024
-ROW = 1024
-WARM = 20
+V_FIRST = 1536
+ROW = 640
 
 FLOPS = 2 * 128 * 512 * 1024 + 2 * 128 * 512 * 128
 BYTES = 2 * 128 * 2048 * 4 + 2 * 16 * 2048 + 2048 * 4 + 2 * 128 * 128 * 4 + 2 * 16 * 128 + 128 * 32 * 2 + 128 * 128 * 4
@@ -47,22 +46,18 @@ def tile_attend_rel2_cap_srtq128n512t2048_kernel(tc, q_words, q_scales, k_words,
         ks_pool = sb.tile([P, T], U8, name="ks_pool", align_bytes=64)
         kw_pool = sb.tile([P, T], I32, name="kw_pool", align_bytes=64)
         v_pool = sb.tile([P, T], F32, name="v_pool", tag="values", align_bytes=64)
-        vs_pool = sb.tile([P, T], F32, name="vs_pool", tag="reused", align_bytes=64)
+        vs_pool = sb.tile([P, T], F32, name="vs_pool", align_bytes=64)
         q_codes = sb.tile([P, PASSES, P], I32, name="q_codes", align_bytes=64)
         staged = sb.tile([P, ROW], U8, name="staged", align_bytes=64)
         planes = sb.tile([P, PASSES, ROW], U8, name="planes", align_bytes=64)
         ident = sb.tile([P, P], F32, name="ident", align_bytes=64)
 
         warm = sb.tile([P, 2], F32, name="warm")
+        nc.vector.memset(warm[:, 0:1], 0.0)
+        nc.vector.memset(ident[:], 0.0)
+        make_identity(nc, ident[:], nomemset=True)
+        nc.vector.memset(ks_pool[0:KS_ROW, :].bitcast(I32), 0)
         nc.vector.memset(vs_pool[0:VS_ROW, :].bitcast(I32), 0)
-        nc.gpsimd.memset(warm[:, 0:1], 0.0)
-        nc.gpsimd.memset(ks_pool[0:KS_ROW, :].bitcast(I32), 0)
-        nc.gpsimd.memset(staged[:, N + P :].bitcast(I32), 0)
-        nc.gpsimd.memset(planes[:, :, 0 : N + P].bitcast(I32), 0)
-        make_identity(nc, ident[:])
-        warm_ps = ps.tile([P, P], F32, name="warm_ps")
-        for i in range(WARM):
-            nc.tensor.matmul(warm_ps[:], lhsT=ident[:], rhs=ident[:], is_transpose=True, start=(i == 0), stop=(i == WARM - 1))
 
         nc.sync.dma_start(offsets[:], offs)
         nc.scalar.dma_start(ks_pool[KS_ROW:, :].bitcast(I32), k_scales.rearrange("o f t -> f o t").bitcast(I32))
@@ -75,6 +70,7 @@ def tile_attend_rel2_cap_srtq128n512t2048_kernel(tc, q_words, q_scales, k_words,
 
         ks_rows = sb.tile([P, N], U8, name="ks_rows", align_bytes=64)
         nc.vector.tensor_copy(ks_rows[:], ks_pool[:].indirect(offsets[:]))
+        nc.vector.memset(planes[:].bitcast(I32), 0)
         nc.vector.tensor_copy(places(staged[:, 0:N]), by_place(ks_rows[:]))
         for quad in range(4):
             queue = nc.scalar if quad < 2 else nc.sync
@@ -94,7 +90,7 @@ def tile_attend_rel2_cap_srtq128n512t2048_kernel(tc, q_words, q_scales, k_words,
         vs_slot = sb.tile([P, 1, PACK], F32, name="vs_slot")
         nc.scalar.copy(vs_slot[:, 0, :], vs_ps[:, :, VS_ROW])
 
-        k_pairs = sb.tile([P, N], U32, name="k_pairs", tag="reused", align_bytes=64)
+        k_pairs = sb.tile([P, N], U32, name="k_pairs", align_bytes=64)
         nc.vector.tensor_copy(k_pairs[:], kw_pool[:].bitcast(U32).indirect(offsets[:]))
         halves = k_pairs[:].bitcast(U16).rearrange("p (j u r e o) -> p u e o j r", u=2, r=RUN, e=2, o=PASSES)
         th = sb.tile([P, PACK, P], F32, name="th", align_bytes=64)

@@ -9,8 +9,10 @@ PACK = 4
 RUN = 8
 CAP = 2.0
 VS_ROW = 127
-KS_ROW = 96
-V_FIRST = 1536
+KS_ROWS = 32
+V_FIRST = 1280
+HALF = N // 2
+V_HALF = T - N + HALF
 ROW = 640
 
 FLOPS = 2 * 128 * 512 * 1024 + 2 * 128 * 512 * 128
@@ -56,13 +58,14 @@ def tile_attend_rel2_cap_srtq128n512t2048_kernel(tc, q_words, q_scales, k_words,
         nc.vector.memset(warm[:, 0:1], 0.0)
         nc.vector.memset(ident[:], 0.0)
         make_identity(nc, ident[:], nomemset=True)
-        nc.vector.memset(ks_pool[0:KS_ROW, :].bitcast(I32), 0)
+        nc.vector.memset(ks_pool[KS_ROWS:64, :].bitcast(I32), 0)
+        nc.vector.memset(ks_pool[64:, :].bitcast(I32), 0)
         nc.vector.memset(vs_pool[0:VS_ROW, :].bitcast(I32), 0)
 
         nc.sync.dma_start(offsets[:], offs)
-        nc.scalar.dma_start(ks_pool[KS_ROW:, :].bitcast(I32), k_scales.rearrange("o f t -> f o t").bitcast(I32))
+        nc.scalar.dma_start(ks_pool[0:KS_ROWS, :].bitcast(I32), k_scales.rearrange("o f t -> f o t").bitcast(I32))
         nc.sync.dma_start(vs_pool[VS_ROW:, :], vs[0:1, :])
-        nc.scalar.dma_start(staged[KS_ROW:, N : N + P].bitcast(I32), q_scales[0].rearrange("o f q -> f o q").bitcast(I32))
+        nc.scalar.dma_start(staged[0:KS_ROWS, N : N + P].bitcast(I32), q_scales[0].rearrange("o f q -> f o q").bitcast(I32))
         nc.sync.dma_start(kw_pool[:], k_words[0].rearrange("g t b -> g (t b)").bitcast(I32))
         nc.sync.dma_start(q_codes[:], q_words[0].rearrange("o g q r -> g o (q r)").bitcast(I32))
         nc.sync.dma_start(v_pool[:, 0:V_FIRST], vT[:, 0:V_FIRST])
@@ -76,9 +79,10 @@ def tile_attend_rel2_cap_srtq128n512t2048_kernel(tc, q_words, q_scales, k_words,
             queue = nc.scalar if quad < 2 else nc.sync
             queue.dma_start(
                 planes[32 * quad : 32 * quad + 4, :, :].bitcast(I32),
-                staged[KS_ROW + 8 * quad : KS_ROW + 8 * quad + 8, :].bitcast(I32),
+                staged[8 * quad : 8 * quad + 8, :].bitcast(I32),
             )
-        nc.sync.dma_start(v_pool[:, V_FIRST:], vT[:, V_FIRST:])
+        nc.sync.dma_start(v_pool[:, V_FIRST:V_HALF], vT[:, V_FIRST:V_HALF])
+        nc.sync.dma_start(v_pool[:, V_HALF:], vT[:, V_HALF:])
 
         vs_rows = sb.tile([P, N], F32, name="vs_rows", align_bytes=64)
         nc.vector.tensor_copy(vs_rows[:], vs_pool[:].indirect(offsets[:]))
@@ -111,21 +115,29 @@ def tile_attend_rel2_cap_srtq128n512t2048_kernel(tc, q_words, q_scales, k_words,
             nc.scalar.activation(th[:, t, :], score[:], ACT.Tanh, scale=1.0 / CAP)
 
         v_rows = sb.tile([P, 2, N // 2], BF16, name="v_rows", align_bytes=64)
-        nc.vector.tensor_copy(v_rows[:].rearrange("p u (j s) -> p j u s", s=2 * RUN), v_pool[:].indirect(offsets[:]))
-        v_ps = ps.tile([P, 2, P], F32, name="v_ps", tag=f"bank{PACK - 1}")
+        v_blocks = v_rows[:].rearrange("p u (j s) -> p j u s", s=2 * RUN)
+        nc.vector.tensor_copy(v_blocks[:, 0:8], v_pool[:, 0:V_HALF].indirect(offsets[:, 0 : HALF // 16]))
+        nc.vector.tensor_copy(v_blocks[:, 8:16], v_pool[:].indirect(offsets[:, HALF // 16 :]))
+        v_ps = ps.tile([P, 2, P], F32, name="v_ps", tag=f"bank{PACK - 2}")
         for u in range(2):
             nc.tensor.transpose(v_ps[:, u, :], v_rows[:, u, :].bitcast(F32), ident[:])
         v_bf = sb.tile([P, P * PACK], BF16, name="v_bf", align_bytes=64)
         nc.scalar.copy(v_bf[:].bitcast(F32).rearrange("p (f u) -> p f u", u=2), v_ps[:].rearrange("p u f -> p f u"))
 
         sq = sb.tile([P, PACK, P], F32, name="sq", tag="values", align_bytes=64)
-        for first, last in ((0, 2), (2, 3), (3, 4)):
-            part = th[:, first:last, :]
-            nc.vector.scalar_tensor_tensor(sq[:, first:last, :], part, 0.0, part, ALU.max, ALU.mult)
+        query_halves = (slice(0, P // 2), slice(P // 2, P))
+        for qs in query_halves:
+            nc.vector.scalar_tensor_tensor(sq[:, :, qs], th[:, :, qs], 0.0, th[:, :, qs], ALU.max, ALU.mult)
         w_bf = sb.tile([P, P, PACK], BF16, name="w_bf", tag="weights", align_bytes=64)
-        nc.vector.scalar_tensor_tensor(
-            w_bf[:], sq[:].rearrange("p t q -> p q t"), CAP * CAP, vs_slot[:].to_broadcast([P, P, PACK]), ALU.mult, ALU.mult
-        )
+        for qs in query_halves:
+            nc.vector.scalar_tensor_tensor(
+                w_bf[:, qs, :],
+                sq[:, :, qs].rearrange("p t q -> p q t"),
+                CAP * CAP,
+                vs_slot[:].to_broadcast([P, P // 2, PACK]),
+                ALU.mult,
+                ALU.mult,
+            )
 
         l_ps = ps.tile([P, P], F32, name="l_ps")
         for t in range(PACK):
@@ -138,8 +150,8 @@ def tile_attend_rel2_cap_srtq128n512t2048_kernel(tc, q_words, q_scales, k_words,
         w_plane = sb.tile([P, P], U8, name="w_plane", align_bytes=64)
         v_codes = sb.tile([P, P], U32, name="v_codes", align_bytes=64)
         v_plane = sb.tile([P, P], U8, name="v_plane", align_bytes=64)
-        nc.vector.quantize_mx(out=v_codes[:].bitcast(FP8X4), scales=v_plane[:], in_=v_bf[:])
         nc.vector.quantize_mx(out=w_codes[:].bitcast(FP8X4), scales=w_plane[:], in_=w_bf[:].rearrange("p q t -> p (q t)"))
+        nc.vector.quantize_mx(out=v_codes[:].bitcast(FP8X4), scales=v_plane[:], in_=v_bf[:])
         inv = sb.tile([P, 1], F32, name="inv", tag="weights", align_bytes=64)
         nc.vector.reciprocal(inv[:], total[:])
 

@@ -9,7 +9,7 @@ PACK = 4
 RUN = 8
 CAP = 2.0
 VS_ROW = 127
-KS_ROWS = 32
+KS_ROW = 96
 V_FIRST = 1280
 HALF = N // 2
 V_HALF = T - N + HALF
@@ -55,17 +55,14 @@ def tile_attend_rel2_cap_srtq128n512t2048_kernel(tc, q_words, q_scales, k_words,
         ident = sb.tile([P, P], F32, name="ident", align_bytes=64)
 
         warm = sb.tile([P, 2], F32, name="warm")
-        nc.vector.memset(warm[:, 0:1], 0.0)
-        nc.vector.memset(ident[:], 0.0)
-        make_identity(nc, ident[:], nomemset=True)
-        nc.vector.memset(ks_pool[KS_ROWS:64, :].bitcast(I32), 0)
-        nc.vector.memset(ks_pool[64:, :].bitcast(I32), 0)
+        nc.gpsimd.memset(warm[:, 0:1], 0.0)
+        nc.vector.memset(ks_pool[0:KS_ROW, :].bitcast(I32), 0)
         nc.vector.memset(vs_pool[0:VS_ROW, :].bitcast(I32), 0)
 
         nc.sync.dma_start(offsets[:], offs)
-        nc.scalar.dma_start(ks_pool[0:KS_ROWS, :].bitcast(I32), k_scales.rearrange("o f t -> f o t").bitcast(I32))
+        nc.scalar.dma_start(ks_pool[KS_ROW:, :].bitcast(I32), k_scales.rearrange("o f t -> f o t").bitcast(I32))
         nc.sync.dma_start(vs_pool[VS_ROW:, :], vs[0:1, :])
-        nc.scalar.dma_start(staged[0:KS_ROWS, N : N + P].bitcast(I32), q_scales[0].rearrange("o f q -> f o q").bitcast(I32))
+        nc.scalar.dma_start(staged[KS_ROW:, N : N + P].bitcast(I32), q_scales[0].rearrange("o f q -> f o q").bitcast(I32))
         nc.sync.dma_start(kw_pool[:], k_words[0].rearrange("g t b -> g (t b)").bitcast(I32))
         nc.sync.dma_start(q_codes[:], q_words[0].rearrange("o g q r -> g o (q r)").bitcast(I32))
         nc.sync.dma_start(v_pool[:, 0:V_FIRST], vT[:, 0:V_FIRST])
@@ -73,13 +70,15 @@ def tile_attend_rel2_cap_srtq128n512t2048_kernel(tc, q_words, q_scales, k_words,
 
         ks_rows = sb.tile([P, N], U8, name="ks_rows", align_bytes=64)
         nc.vector.tensor_copy(ks_rows[:], ks_pool[:].indirect(offsets[:]))
+        nc.vector.memset(ident[:], 0.0)
         nc.vector.memset(planes[:].bitcast(I32), 0)
+        make_identity(nc, ident[:], nomemset=True)
         nc.vector.tensor_copy(places(staged[:, 0:N]), by_place(ks_rows[:]))
         for quad in range(4):
             queue = nc.scalar if quad < 2 else nc.sync
             queue.dma_start(
                 planes[32 * quad : 32 * quad + 4, :, :].bitcast(I32),
-                staged[8 * quad : 8 * quad + 8, :].bitcast(I32),
+                staged[KS_ROW + 8 * quad : KS_ROW + 8 * quad + 8, :].bitcast(I32),
             )
         nc.sync.dma_start(v_pool[:, V_FIRST:V_HALF], vT[:, V_FIRST:V_HALF])
         nc.sync.dma_start(v_pool[:, V_HALF:], vT[:, V_HALF:])

@@ -91,56 +91,60 @@ def tile_attend_rel2_cap_srtq128n512t2048_kernel(tc, q_words, q_scales, k_words,
         for t in range(PACK):
             nc.tensor.transpose(vs_ps[:, t, :], vs_placed[:, t * P : (t + 1) * P], ident[:])
         vs_slot = sb.tile([P, 1, PACK], F32, name="vs_slot")
-        nc.scalar.copy(vs_slot[:, 0, :], vs_ps[:, :, VS_ROW])
+        nc.scalar.activation(vs_slot[:, 0, :], vs_ps[:, :, VS_ROW], ACT.Copy, scale=CAP * CAP)
 
         k_pairs = sb.tile([P, N], U32, name="k_pairs", align_bytes=64)
         nc.vector.tensor_copy(k_pairs[:], kw_pool[:].bitcast(U32).indirect(offsets[:]))
         halves = k_pairs[:].bitcast(U16).rearrange("p (j u r e o) -> p u e o j r", u=2, r=RUN, e=2, o=PASSES)
-        th = sb.tile([P, PACK, P], F32, name="th", align_bytes=64)
-        for t in range(PACK):
-            k_codes = sb.tile([P, PASSES, 2 * P], U8, name=f"k_codes{t}", align_bytes=64)
-            nc.vector.tensor_copy(k_codes[:].bitcast(U16).rearrange("p o (j r) -> p o j r", r=RUN), halves[:, t // 2, t % 2])
-            score = ps.tile([P, P], F32, name=f"score{t}", tag=f"bank{t}")
-            for o in range(PASSES):
-                nc.tensor.matmul_mx(
-                    out=score[:],
-                    lhsT=k_codes[:, o, :].bitcast(FP4X4),
-                    lhsT_scale=planes[:, o, t * P : (t + 1) * P],
-                    rhs=q_codes[:, o, :].bitcast(FP8X4),
-                    rhs_scale=planes[:, o, N : N + P],
-                    start=(o == 0),
-                    stop=(o == PASSES - 1),
-                )
-            nc.scalar.activation(th[:, t, :], score[:], ACT.Tanh, scale=1.0 / CAP)
+        query_halves = (slice(0, P // 2), slice(P // 2, P))
+        th = sb.tile([P, 2, P, 2], F32, name="th", align_bytes=64)
+        for u in range(2):
+            scores = ps.tile([P, 2, P], F32, name=f"scores{u}", tag=f"bank{u}")
+            for e in range(2):
+                t = 2 * u + e
+                k_codes = sb.tile([P, PASSES, 2 * P], U8, name=f"k_codes{t}", align_bytes=64)
+                nc.vector.tensor_copy(k_codes[:].bitcast(U16).rearrange("p o (j r) -> p o j r", r=RUN), halves[:, u, e])
+                for o in range(PASSES):
+                    nc.tensor.matmul_mx(
+                        out=scores[:, e, :],
+                        lhsT=k_codes[:, o, :].bitcast(FP4X4),
+                        lhsT_scale=planes[:, o, t * P : (t + 1) * P],
+                        rhs=q_codes[:, o, :].bitcast(FP8X4),
+                        rhs_scale=planes[:, o, N : N + P],
+                        start=(o == 0),
+                        stop=(o == PASSES - 1),
+                    )
+            for qs in query_halves:
+                nc.scalar.activation(th[:, u, qs, :], scores[:, :, qs].rearrange("p e q -> p q e"), ACT.Tanh, scale=1.0 / CAP)
 
         v_rows = sb.tile([P, 2, N // 2], BF16, name="v_rows", align_bytes=64)
         v_blocks = v_rows[:].rearrange("p u (j s) -> p j u s", s=2 * RUN)
         nc.vector.tensor_copy(v_blocks[:, 0:8], v_pool[:, 0:V_HALF].indirect(offsets[:, 0 : HALF // 16]))
         nc.vector.tensor_copy(v_blocks[:, 8:16], v_pool[:].indirect(offsets[:, HALF // 16 :]))
-        v_ps = ps.tile([P, 2, P], F32, name="v_ps", tag=f"bank{PACK - 2}")
+        v_ps = ps.tile([P, 2, P], F32, name="v_ps", tag="bank0")
         for u in range(2):
             nc.tensor.transpose(v_ps[:, u, :], v_rows[:, u, :].bitcast(F32), ident[:])
         v_bf = sb.tile([P, P * PACK], BF16, name="v_bf", align_bytes=64)
         nc.scalar.copy(v_bf[:].bitcast(F32).rearrange("p (f u) -> p f u", u=2), v_ps[:].rearrange("p u f -> p f u"))
 
-        sq = sb.tile([P, PACK, P], F32, name="sq", tag="values", align_bytes=64)
-        query_halves = (slice(0, P // 2), slice(P // 2, P))
+        sq = sb.tile([P, 2, P, 2], F32, name="sq", tag="values", align_bytes=64)
+        for u, qs in ((0, slice(0, P)), (1, query_halves[0]), (1, query_halves[1])):
+            part = th[:, u, qs, :]
+            nc.vector.scalar_tensor_tensor(sq[:, u, qs, :], part, 0.0, part, ALU.max, ALU.mult)
+        w_bf = sb.tile([P, P, 2, 2], BF16, name="w_bf", tag="weights", align_bytes=64)
         for qs in query_halves:
-            nc.vector.scalar_tensor_tensor(sq[:, :, qs], th[:, :, qs], 0.0, th[:, :, qs], ALU.max, ALU.mult)
-        w_bf = sb.tile([P, P, PACK], BF16, name="w_bf", tag="weights", align_bytes=64)
-        for qs in query_halves:
-            nc.vector.scalar_tensor_tensor(
-                w_bf[:, qs, :],
-                sq[:, :, qs].rearrange("p t q -> p q t"),
-                CAP * CAP,
-                vs_slot[:].to_broadcast([P, P // 2, PACK]),
-                ALU.mult,
+            nc.vector.tensor_tensor(
+                w_bf[:, qs],
+                sq[:, :, qs, :].rearrange("p u q e -> p q u e"),
+                vs_slot[:].rearrange("p one (u e) -> p one u e", e=2).to_broadcast([P, P // 2, 2, 2]),
                 ALU.mult,
             )
 
         l_ps = ps.tile([P, P], F32, name="l_ps")
         for t in range(PACK):
-            nc.tensor.matmul(l_ps[:], lhsT=sq[:, t, :], rhs=ident[:], is_transpose=True, start=(t == 0), stop=(t == PACK - 1))
+            nc.tensor.matmul(
+                l_ps[:], lhsT=sq[:, t // 2, :, t % 2], rhs=ident[:], is_transpose=True, start=(t == 0), stop=(t == PACK - 1)
+            )
         l_terms = sb.tile([P, P], F32, name="l_terms")
         total = sb.tile([P, 1], F32, name="total")
         nc.scalar.activation(l_terms[:], l_ps[:], ACT.Copy, scale=CAP * CAP, bias=1.0 / P, accum_out=total[:])
@@ -149,7 +153,7 @@ def tile_attend_rel2_cap_srtq128n512t2048_kernel(tc, q_words, q_scales, k_words,
         w_plane = sb.tile([P, P], U8, name="w_plane", align_bytes=64)
         v_codes = sb.tile([P, P], U32, name="v_codes", align_bytes=64)
         v_plane = sb.tile([P, P], U8, name="v_plane", align_bytes=64)
-        nc.vector.quantize_mx(out=w_codes[:].bitcast(FP8X4), scales=w_plane[:], in_=w_bf[:].rearrange("p q t -> p (q t)"))
+        nc.vector.quantize_mx(out=w_codes[:].bitcast(FP8X4), scales=w_plane[:], in_=w_bf[:].rearrange("p q u e -> p (q u e)"))
         nc.vector.quantize_mx(out=v_codes[:].bitcast(FP8X4), scales=v_plane[:], in_=v_bf[:])
         inv = sb.tile([P, 1], F32, name="inv", tag="weights", align_bytes=64)
         nc.vector.reciprocal(inv[:], total[:])

@@ -10,7 +10,7 @@ RUN = 8
 CAP = 2.0
 VS_ROW = 127
 KS_ROW = 96
-V_FIRST = 1280
+V_FIRST = 1152
 HALF = N // 2
 V_HALF = T - N + HALF
 ROW = 640
@@ -54,10 +54,11 @@ def tile_attend_rel2_cap_srtq128n512t2048_kernel(tc, q_words, q_scales, k_words,
         planes = sb.tile([P, PASSES, ROW], U8, name="planes", align_bytes=64)
         ident = sb.tile([P, P], F32, name="ident", align_bytes=64)
 
-        warm = sb.tile([P, 2], F32, name="warm")
-        nc.gpsimd.memset(warm[:, 0:1], 0.0)
+        zero = sb.tile([P, 1], F32, name="zero")
+        nc.gpsimd.memset(zero[:], 0.0)
         nc.vector.memset(ks_pool[0:KS_ROW, :].bitcast(I32), 0)
         nc.vector.memset(vs_pool[0:VS_ROW, :].bitcast(I32), 0)
+        nc.vector.memset(planes[:].bitcast(I32), 0)
 
         nc.sync.dma_start(offsets[:], offs)
         nc.scalar.dma_start(ks_pool[KS_ROW:, :].bitcast(I32), k_scales.rearrange("o f t -> f o t").bitcast(I32))
@@ -66,13 +67,13 @@ def tile_attend_rel2_cap_srtq128n512t2048_kernel(tc, q_words, q_scales, k_words,
         nc.sync.dma_start(kw_pool[:], k_words[0].rearrange("g t b -> g (t b)").bitcast(I32))
         nc.sync.dma_start(q_codes[:], q_words[0].rearrange("o g q r -> g o (q r)").bitcast(I32))
         nc.sync.dma_start(v_pool[:, 0:V_FIRST], vT[:, 0:V_FIRST])
-        nc.scalar.activation(warm[:, 1:2], warm[:, 0:1], ACT.Tanh)
-
-        ks_rows = sb.tile([P, N], U8, name="ks_rows", align_bytes=64)
-        nc.vector.tensor_copy(ks_rows[:], ks_pool[:].indirect(offsets[:]))
-        nc.vector.memset(ident[:], 0.0)
-        nc.vector.memset(planes[:].bitcast(I32), 0)
+        nc.scalar.activation(ident[:], zero[:].to_broadcast([P, P]), ACT.Copy)
         make_identity(nc, ident[:], nomemset=True)
+
+        ks_rows = sb.tile([P, N], U8, name="ks_rows", tag="gathered", align_bytes=64)
+        nc.vector.tensor_copy(ks_rows[:], ks_pool[:].indirect(offsets[:]))
+        vs_rows = sb.tile([P, N], F32, name="vs_rows", align_bytes=64)
+        nc.vector.tensor_copy(vs_rows[:, 0:HALF], vs_pool[:].indirect(offsets[:, 0 : HALF // 16]))
         nc.vector.tensor_copy(places(staged[:, 0:N]), by_place(ks_rows[:]))
         for quad in range(4):
             queue = nc.scalar if quad < 2 else nc.sync
@@ -83,17 +84,17 @@ def tile_attend_rel2_cap_srtq128n512t2048_kernel(tc, q_words, q_scales, k_words,
         nc.sync.dma_start(v_pool[:, V_FIRST:V_HALF], vT[:, V_FIRST:V_HALF])
         nc.sync.dma_start(v_pool[:, V_HALF:], vT[:, V_HALF:])
 
-        vs_rows = sb.tile([P, N], F32, name="vs_rows", align_bytes=64)
-        nc.vector.tensor_copy(vs_rows[:], vs_pool[:].indirect(offsets[:]))
+        nc.vector.tensor_copy(vs_rows[:, HALF:], vs_pool[:].indirect(offsets[:, HALF // 16 :]))
         vs_placed = sb.tile([P, N], F32, name="vs_placed", align_bytes=64)
-        nc.scalar.copy(places(vs_placed[:]), by_place(vs_rows[:]))
+        for blocks in (slice(0, 8), slice(8, 16)):
+            nc.scalar.copy(places(vs_placed[:])[:, :, :, blocks], by_place(vs_rows[:])[:, :, :, blocks])
         vs_ps = ps.tile([P, PACK, P], F32, name="vs_ps")
         for t in range(PACK):
             nc.tensor.transpose(vs_ps[:, t, :], vs_placed[:, t * P : (t + 1) * P], ident[:])
         vs_slot = sb.tile([P, 1, PACK], F32, name="vs_slot")
         nc.scalar.activation(vs_slot[:, 0, :], vs_ps[:, :, VS_ROW], ACT.Copy, scale=CAP * CAP)
 
-        k_pairs = sb.tile([P, N], U32, name="k_pairs", align_bytes=64)
+        k_pairs = sb.tile([P, N], U32, name="k_pairs", tag="gathered", align_bytes=64)
         nc.vector.tensor_copy(k_pairs[:], kw_pool[:].bitcast(U32).indirect(offsets[:]))
         halves = k_pairs[:].bitcast(U16).rearrange("p (j u r e o) -> p u e o j r", u=2, r=RUN, e=2, o=PASSES)
         query_halves = (slice(0, P // 2), slice(P // 2, P))
@@ -153,8 +154,11 @@ def tile_attend_rel2_cap_srtq128n512t2048_kernel(tc, q_words, q_scales, k_words,
         w_plane = sb.tile([P, P], U8, name="w_plane", align_bytes=64)
         v_codes = sb.tile([P, P], U32, name="v_codes", align_bytes=64)
         v_plane = sb.tile([P, P], U8, name="v_plane", align_bytes=64)
-        nc.vector.quantize_mx(out=w_codes[:].bitcast(FP8X4), scales=w_plane[:], in_=w_bf[:].rearrange("p q u e -> p (q u e)"))
+        w_flat = w_bf[:].rearrange("p q u e -> p (q u e)")
+        first, second = query_halves
+        nc.vector.quantize_mx(out=w_codes[:, first].bitcast(FP8X4), scales=w_plane[:, first], in_=w_flat[:, 0 : N // 2])
         nc.vector.quantize_mx(out=v_codes[:].bitcast(FP8X4), scales=v_plane[:], in_=v_bf[:])
+        nc.vector.quantize_mx(out=w_codes[:, second].bitcast(FP8X4), scales=w_plane[:, second], in_=w_flat[:, N // 2 :])
         inv = sb.tile([P, 1], F32, name="inv", tag="weights", align_bytes=64)
         nc.vector.reciprocal(inv[:], total[:])
 

@@ -70,11 +70,13 @@ def tile_attend_rel2_cap_srtq128n512t2048_kernel(tc, q_words, q_scales, k_words,
         nc.scalar.activation(ident[:], zero[:].to_broadcast([P, P]), ACT.Copy)
         make_identity(nc, ident[:], nomemset=True)
 
-        ks_rows = sb.tile([P, N], U8, name="ks_rows", tag="gathered", align_bytes=64)
-        nc.vector.tensor_copy(ks_rows[:], ks_pool[:].indirect(offsets[:]))
-        vs_rows = sb.tile([P, N], F32, name="vs_rows", align_bytes=64)
-        nc.vector.tensor_copy(vs_rows[:, 0:HALF], vs_pool[:].indirect(offsets[:, 0 : HALF // 16]))
-        nc.vector.tensor_copy(places(staged[:, 0:N]), by_place(ks_rows[:]))
+        ks_rows = []
+        for h, tag in enumerate(("first", "gathered")):
+            rows = sb.tile([P, HALF], U8, name=f"ks_rows{h}", tag=tag, align_bytes=64)
+            nc.vector.tensor_copy(rows[:], ks_pool[:].indirect(offsets[:, h * HALF // 16 : (h + 1) * HALF // 16]))
+            ks_rows.append(rows)
+        for h in range(2):
+            nc.vector.tensor_copy(places(staged[:, 0:N])[:, :, :, 8 * h : 8 * h + 8], by_place(ks_rows[h][:]))
         for quad in range(4):
             queue = nc.scalar if quad < 2 else nc.sync
             queue.dma_start(
@@ -84,10 +86,13 @@ def tile_attend_rel2_cap_srtq128n512t2048_kernel(tc, q_words, q_scales, k_words,
         nc.sync.dma_start(v_pool[:, V_FIRST:V_HALF], vT[:, V_FIRST:V_HALF])
         nc.sync.dma_start(v_pool[:, V_HALF:], vT[:, V_HALF:])
 
+        vs_rows = sb.tile([P, N], F32, name="vs_rows", tag="first", align_bytes=64)
+        nc.vector.tensor_copy(vs_rows[:, 0:HALF], vs_pool[:].indirect(offsets[:, 0 : HALF // 16]))
         nc.vector.tensor_copy(vs_rows[:, HALF:], vs_pool[:].indirect(offsets[:, HALF // 16 :]))
         vs_placed = sb.tile([P, N], F32, name="vs_placed", align_bytes=64)
-        for blocks in (slice(0, 8), slice(8, 16)):
-            nc.scalar.copy(places(vs_placed[:])[:, :, :, blocks], by_place(vs_rows[:])[:, :, :, blocks])
+        nc.scalar.copy(places(vs_placed[:])[:, :, :, 0:8], by_place(vs_rows[:])[:, :, :, 0:8])
+        for u in range(2):
+            nc.scalar.copy(places(vs_placed[:])[:, u, :, 8:16], by_place(vs_rows[:])[:, u, :, 8:16])
         vs_ps = ps.tile([P, PACK, P], F32, name="vs_ps")
         for t in range(PACK):
             nc.tensor.transpose(vs_ps[:, t, :], vs_placed[:, t * P : (t + 1) * P], ident[:])
@@ -95,20 +100,24 @@ def tile_attend_rel2_cap_srtq128n512t2048_kernel(tc, q_words, q_scales, k_words,
         nc.scalar.activation(vs_slot[:, 0, :], vs_ps[:, :, VS_ROW], ACT.Copy, scale=CAP * CAP)
 
         k_pairs = sb.tile([P, N], U32, name="k_pairs", tag="gathered", align_bytes=64)
-        nc.vector.tensor_copy(k_pairs[:], kw_pool[:].bitcast(U32).indirect(offsets[:]))
-        halves = k_pairs[:].bitcast(U16).rearrange("p (j u r e o) -> p u e o j r", u=2, r=RUN, e=2, o=PASSES)
+        nc.vector.tensor_copy(k_pairs[:, 0:HALF], kw_pool[:].bitcast(U32).indirect(offsets[:, 0 : HALF // 16]))
+        nc.vector.tensor_copy(k_pairs[:, HALF:], kw_pool[:].bitcast(U32).indirect(offsets[:, HALF // 16 :]))
+        halves = k_pairs[:].bitcast(U16).rearrange("p (j u r c) -> p u c j r", u=2, r=RUN, c=2 * PASSES)
+        k_codes = sb.tile([P, PACK * PASSES * 2 * P], U8, name="k_codes", align_bytes=64)
+        parted = k_codes[:].bitcast(U16).rearrange("p (u c j r) -> p u c j r", u=2, c=2 * PASSES, r=RUN)
+        nc.vector.tensor_copy(parted[:, :, :, 0:8], halves[:, :, :, 0:8])
         query_halves = (slice(0, P // 2), slice(P // 2, P))
         th = sb.tile([P, 2, P, 2], F32, name="th", align_bytes=64)
         for u in range(2):
             scores = ps.tile([P, 2, P], F32, name=f"scores{u}", tag=f"bank{u}")
             for e in range(2):
                 t = 2 * u + e
-                k_codes = sb.tile([P, PASSES, 2 * P], U8, name=f"k_codes{t}", align_bytes=64)
-                nc.vector.tensor_copy(k_codes[:].bitcast(U16).rearrange("p o (j r) -> p o j r", r=RUN), halves[:, u, e])
+                both = slice(PASSES * e, PASSES * (e + 1))
+                nc.vector.tensor_copy(parted[:, u, both, 8:16], halves[:, u, both, 8:16])
                 for o in range(PASSES):
                     nc.tensor.matmul_mx(
                         out=scores[:, e, :],
-                        lhsT=k_codes[:, o, :].bitcast(FP4X4),
+                        lhsT=k_codes[:, (PASSES * t + o) * 2 * P : (PASSES * t + o + 1) * 2 * P].bitcast(FP4X4),
                         lhsT_scale=planes[:, o, t * P : (t + 1) * P],
                         rhs=q_codes[:, o, :].bitcast(FP8X4),
                         rhs_scale=planes[:, o, N : N + P],

@@ -10,7 +10,7 @@ RUN = 8
 CAP = 2.0
 VS_ROW = 127
 KS_ROW = 96
-V_FIRST = 1152
+V_FIRST = 896
 HALF = N // 2
 V_HALF = T - N + HALF
 ROW = 640
@@ -64,7 +64,9 @@ def tile_attend_rel2_cap_srtq128n512t2048_kernel(tc, q_words, q_scales, k_words,
         nc.scalar.dma_start(ks_pool[KS_ROW:, :].bitcast(I32), k_scales.rearrange("o f t -> f o t").bitcast(I32))
         nc.sync.dma_start(vs_pool[VS_ROW:, :], vs[0:1, :])
         nc.scalar.dma_start(staged[KS_ROW:, N : N + P].bitcast(I32), q_scales[0].rearrange("o f q -> f o q").bitcast(I32))
-        nc.sync.dma_start(kw_pool[:], k_words[0].rearrange("g t b -> g (t b)").bitcast(I32))
+        kw_words = k_words[0].rearrange("g t b -> g (t b)").bitcast(I32)
+        nc.sync.dma_start(kw_pool[:, 0:V_HALF], kw_words[:, 0:V_HALF])
+        nc.sync.dma_start(kw_pool[:, V_HALF:], kw_words[:, V_HALF:])
         nc.sync.dma_start(q_codes[:], q_words[0].rearrange("o g q r -> g o (q r)").bitcast(I32))
         nc.sync.dma_start(v_pool[:, 0:V_FIRST], vT[:, 0:V_FIRST])
         nc.scalar.activation(ident[:], zero[:].to_broadcast([P, P]), ACT.Copy)
@@ -100,24 +102,21 @@ def tile_attend_rel2_cap_srtq128n512t2048_kernel(tc, q_words, q_scales, k_words,
         nc.scalar.activation(vs_slot[:, 0, :], vs_ps[:, :, VS_ROW], ACT.Copy, scale=CAP * CAP)
 
         k_pairs = sb.tile([P, N], U32, name="k_pairs", tag="gathered", align_bytes=64)
-        nc.vector.tensor_copy(k_pairs[:, 0:HALF], kw_pool[:].bitcast(U32).indirect(offsets[:, 0 : HALF // 16]))
+        nc.vector.tensor_copy(k_pairs[:, 0:HALF], kw_pool[:, 0:V_HALF].bitcast(U32).indirect(offsets[:, 0 : HALF // 16]))
         nc.vector.tensor_copy(k_pairs[:, HALF:], kw_pool[:].bitcast(U32).indirect(offsets[:, HALF // 16 :]))
-        halves = k_pairs[:].bitcast(U16).rearrange("p (j u r c) -> p u c j r", u=2, r=RUN, c=2 * PASSES)
-        k_codes = sb.tile([P, PACK * PASSES * 2 * P], U8, name="k_codes", align_bytes=64)
-        parted = k_codes[:].bitcast(U16).rearrange("p (u c j r) -> p u c j r", u=2, c=2 * PASSES, r=RUN)
-        nc.vector.tensor_copy(parted[:, :, :, 0:8], halves[:, :, :, 0:8])
+        halves = k_pairs[:].bitcast(U16).rearrange("p (j u r e o) -> p u e o j r", u=2, r=RUN, e=2, o=PASSES)
         query_halves = (slice(0, P // 2), slice(P // 2, P))
         th = sb.tile([P, 2, P, 2], F32, name="th", align_bytes=64)
         for u in range(2):
             scores = ps.tile([P, 2, P], F32, name=f"scores{u}", tag=f"bank{u}")
             for e in range(2):
                 t = 2 * u + e
-                both = slice(PASSES * e, PASSES * (e + 1))
-                nc.vector.tensor_copy(parted[:, u, both, 8:16], halves[:, u, both, 8:16])
+                k_codes = sb.tile([P, PASSES, 2 * P], U8, name=f"k_codes{t}", align_bytes=64)
+                nc.vector.tensor_copy(k_codes[:].bitcast(U16).rearrange("p o (j r) -> p o j r", r=RUN), halves[:, u, e])
                 for o in range(PASSES):
                     nc.tensor.matmul_mx(
                         out=scores[:, e, :],
-                        lhsT=k_codes[:, (PASSES * t + o) * 2 * P : (PASSES * t + o + 1) * 2 * P].bitcast(FP4X4),
+                        lhsT=k_codes[:, o, :].bitcast(FP4X4),
                         lhsT_scale=planes[:, o, t * P : (t + 1) * P],
                         rhs=q_codes[:, o, :].bitcast(FP8X4),
                         rhs_scale=planes[:, o, N : N + P],

@@ -10,7 +10,7 @@ RUN = 8
 CAP = 2.0
 VS_ROW = 127
 KS_ROW = 96
-V_FIRST = 896
+V_FIRST = 640
 HALF = N // 2
 V_HALF = T - N + HALF
 ROW = 640

@@ -30,12 +30,12 @@ ACT = mybir.ActivationFunctionType
 ALU = mybir.AluOpType
 
 
-def by_place(rows):
-    return rows.rearrange("p (j u r e) -> p u e j r", u=2, r=RUN, e=2)
+def by_place(rows, run):
+    return rows.rearrange("p (j t r) -> p t j r", t=PACK, r=run)
 
 
-def places(tile):
-    return tile.rearrange("p (u e j r) -> p u e j r", u=2, e=2, r=RUN)
+def places(tile, run):
+    return tile.rearrange("p (t j r) -> p t j r", t=PACK, r=run)
 
 
 def tile_attend_rel2_cap_srtq128n512t2048_kernel(tc, q_words, q_scales, k_words, k_scales, vT, vs, offs, out):
@@ -78,7 +78,9 @@ def tile_attend_rel2_cap_srtq128n512t2048_kernel(tc, q_words, q_scales, k_words,
             nc.vector.tensor_copy(rows[:], ks_pool[:].indirect(offsets[:, h * HALF // 16 : (h + 1) * HALF // 16]))
             ks_rows.append(rows)
         for h in range(2):
-            nc.vector.tensor_copy(places(staged[:, 0:N])[:, :, :, 8 * h : 8 * h + 8], by_place(ks_rows[h][:]))
+            nc.vector.tensor_copy(
+                places(staged[:, 0:N].bitcast(I32), RUN // 4)[:, :, 8 * h : 8 * h + 8], by_place(ks_rows[h][:].bitcast(I32), RUN // 4)
+            )
         for quad in range(4):
             queue = nc.scalar if quad < 2 else nc.sync
             queue.dma_start(
@@ -92,9 +94,9 @@ def tile_attend_rel2_cap_srtq128n512t2048_kernel(tc, q_words, q_scales, k_words,
         nc.vector.tensor_copy(vs_rows[:, 0:HALF], vs_pool[:].indirect(offsets[:, 0 : HALF // 16]))
         nc.vector.tensor_copy(vs_rows[:, HALF:], vs_pool[:].indirect(offsets[:, HALF // 16 :]))
         vs_placed = sb.tile([P, N], F32, name="vs_placed", align_bytes=64)
-        nc.scalar.copy(places(vs_placed[:])[:, :, :, 0:8], by_place(vs_rows[:])[:, :, :, 0:8])
+        nc.scalar.copy(places(vs_placed[:], RUN)[:, :, 0:8], by_place(vs_rows[:], RUN)[:, :, 0:8])
         for u in range(2):
-            nc.scalar.copy(places(vs_placed[:])[:, u, :, 8:16], by_place(vs_rows[:])[:, u, :, 8:16])
+            nc.scalar.copy(places(vs_placed[:], RUN)[:, 2 * u : 2 * u + 2, 8:16], by_place(vs_rows[:], RUN)[:, 2 * u : 2 * u + 2, 8:16])
         vs_ps = ps.tile([P, PACK, P], F32, name="vs_ps")
         for t in range(PACK):
             nc.tensor.transpose(vs_ps[:, t, :], vs_placed[:, t * P : (t + 1) * P], ident[:])
@@ -104,7 +106,7 @@ def tile_attend_rel2_cap_srtq128n512t2048_kernel(tc, q_words, q_scales, k_words,
         k_pairs = sb.tile([P, N], U32, name="k_pairs", tag="gathered", align_bytes=64)
         nc.vector.tensor_copy(k_pairs[:, 0:HALF], kw_pool[:, 0:V_HALF].bitcast(U32).indirect(offsets[:, 0 : HALF // 16]))
         nc.vector.tensor_copy(k_pairs[:, HALF:], kw_pool[:].bitcast(U32).indirect(offsets[:, HALF // 16 :]))
-        halves = k_pairs[:].bitcast(U16).rearrange("p (j u r e o) -> p u e o j r", u=2, r=RUN, e=2, o=PASSES)
+        halves = k_pairs[:].bitcast(U16).rearrange("p (j t r o) -> p t o j r", t=PACK, r=RUN, o=PASSES)
         query_halves = (slice(0, P // 2), slice(P // 2, P))
         th = sb.tile([P, 2, P, 2], F32, name="th", align_bytes=64)
         for u in range(2):
@@ -112,7 +114,7 @@ def tile_attend_rel2_cap_srtq128n512t2048_kernel(tc, q_words, q_scales, k_words,
             for e in range(2):
                 t = 2 * u + e
                 k_codes = sb.tile([P, PASSES, 2 * P], U8, name=f"k_codes{t}", align_bytes=64)
-                nc.vector.tensor_copy(k_codes[:].bitcast(U16).rearrange("p o (j r) -> p o j r", r=RUN), halves[:, u, e])
+                nc.vector.tensor_copy(k_codes[:].bitcast(U16).rearrange("p o (j r) -> p o j r", r=RUN), halves[:, t])
                 for o in range(PASSES):
                     nc.tensor.matmul_mx(
                         out=scores[:, e, :],
@@ -127,7 +129,7 @@ def tile_attend_rel2_cap_srtq128n512t2048_kernel(tc, q_words, q_scales, k_words,
                 nc.scalar.activation(th[:, u, qs, :], scores[:, :, qs].rearrange("p e q -> p q e"), ACT.Tanh, scale=1.0 / CAP)
 
         v_rows = sb.tile([P, 2, N // 2], BF16, name="v_rows", align_bytes=64)
-        v_blocks = v_rows[:].rearrange("p u (j s) -> p j u s", s=2 * RUN)
+        v_blocks = v_rows[:].rearrange("p u (j r e) -> p j u e r", r=RUN, e=2)
         nc.vector.tensor_copy(v_blocks[:, 0:8], v_pool[:, 0:V_HALF].indirect(offsets[:, 0 : HALF // 16]))
         nc.vector.tensor_copy(v_blocks[:, 8:16], v_pool[:].indirect(offsets[:, HALF // 16 :]))
         v_ps = ps.tile([P, 2, P], F32, name="v_ps", tag="bank0")

@@ -10,7 +10,7 @@ RUN = 8
 CAP = 2.0
 VS_ROW = 127
 KS_ROW = 96
-V_FIRST = 640
+V_FIRST = 960
 HALF = N // 2
 V_HALF = T - N + HALF
 ROW = 640
@@ -81,22 +81,20 @@ def tile_attend_rel2_cap_srtq128n512t2048_kernel(tc, q_words, q_scales, k_words,
             nc.vector.tensor_copy(
                 places(staged[:, 0:N].bitcast(I32), RUN // 4)[:, :, 8 * h : 8 * h + 8], by_place(ks_rows[h][:].bitcast(I32), RUN // 4)
             )
-        for quad in range(4):
-            queue = nc.scalar if quad < 2 else nc.sync
-            queue.dma_start(
+        for quad in (0, 2, 1, 3):
+            nc.sync.dma_start(
                 planes[32 * quad : 32 * quad + 4, :, :].bitcast(I32),
                 staged[KS_ROW + 8 * quad : KS_ROW + 8 * quad + 8, :].bitcast(I32),
             )
         nc.sync.dma_start(v_pool[:, V_FIRST:V_HALF], vT[:, V_FIRST:V_HALF])
         nc.sync.dma_start(v_pool[:, V_HALF:], vT[:, V_HALF:])
 
-        vs_rows = sb.tile([P, N], F32, name="vs_rows", tag="first", align_bytes=64)
-        nc.vector.tensor_copy(vs_rows[:, 0:HALF], vs_pool[:].indirect(offsets[:, 0 : HALF // 16]))
-        nc.vector.tensor_copy(vs_rows[:, HALF:], vs_pool[:].indirect(offsets[:, HALF // 16 :]))
-        vs_placed = sb.tile([P, N], F32, name="vs_placed", align_bytes=64)
-        nc.scalar.copy(places(vs_placed[:], RUN)[:, :, 0:8], by_place(vs_rows[:], RUN)[:, :, 0:8])
-        for u in range(2):
-            nc.scalar.copy(places(vs_placed[:], RUN)[:, 2 * u : 2 * u + 2, 8:16], by_place(vs_rows[:], RUN)[:, 2 * u : 2 * u + 2, 8:16])
+        vs_placed = sb.tile([P, N], F32, name="vs_placed", tag="first", align_bytes=64)
+        vs_blocks = vs_placed[:].bitcast(U32).rearrange("p (t j r) -> p j t r", t=PACK, r=RUN)
+        for h in range(2):
+            nc.vector.tensor_copy(
+                vs_blocks[:, 8 * h : 8 * h + 8], vs_pool[:].bitcast(U32).indirect(offsets[:, h * HALF // 16 : (h + 1) * HALF // 16])
+            )
         vs_ps = ps.tile([P, PACK, P], F32, name="vs_ps")
         for t in range(PACK):
             nc.tensor.transpose(vs_ps[:, t, :], vs_placed[:, t * P : (t + 1) * P], ident[:])

@@ -73,7 +73,7 @@ def tile_attend_rel2_cap_srtq128n512t2048_kernel(tc, q_words, q_scales, k_words,
         make_identity(nc, ident[:], nomemset=True)
 
         ks_rows = []
-        for h, tag in enumerate(("first", "gathered")):
+        for h, tag in enumerate(("gathered", "second")):
             rows = sb.tile([P, HALF], U8, name=f"ks_rows{h}", tag=tag, align_bytes=64)
             nc.vector.tensor_copy(rows[:], ks_pool[:].indirect(offsets[:, h * HALF // 16 : (h + 1) * HALF // 16]))
             ks_rows.append(rows)
@@ -89,12 +89,11 @@ def tile_attend_rel2_cap_srtq128n512t2048_kernel(tc, q_words, q_scales, k_words,
         nc.sync.dma_start(v_pool[:, V_FIRST:V_HALF], vT[:, V_FIRST:V_HALF])
         nc.sync.dma_start(v_pool[:, V_HALF:], vT[:, V_HALF:])
 
-        vs_placed = sb.tile([P, N], F32, name="vs_placed", tag="first", align_bytes=64)
-        vs_blocks = vs_placed[:].bitcast(U32).rearrange("p (t j r) -> p j t r", t=PACK, r=RUN)
-        for h in range(2):
-            nc.vector.tensor_copy(
-                vs_blocks[:, 8 * h : 8 * h + 8], vs_pool[:].bitcast(U32).indirect(offsets[:, h * HALF // 16 : (h + 1) * HALF // 16])
-            )
+        vs_rows = sb.tile([P, N], F32, name="vs_rows", align_bytes=64)
+        nc.scalar.activation(vs_rows[:], vs_pool[:].indirect(offsets[:]), ACT.Copy)
+        vs_placed = sb.tile([P, N], F32, name="vs_placed", align_bytes=64)
+        for u in range(2):
+            nc.scalar.activation(places(vs_placed[:], RUN)[:, 2 * u : 2 * u + 2], by_place(vs_rows[:], RUN)[:, 2 * u : 2 * u + 2], ACT.Copy)
         vs_ps = ps.tile([P, PACK, P], F32, name="vs_ps")
         for t in range(PACK):
             nc.tensor.transpose(vs_ps[:, t, :], vs_placed[:, t * P : (t + 1) * P], ident[:])

@@ -14,6 +14,7 @@ V_FIRST = 960
 HALF = N // 2
 V_HALF = T - N + HALF
 ROW = 640
+FILL_SHARE = 896
 
 FLOPS = 2 * 128 * 512 * 1024 + 2 * 128 * 512 * 128
 BYTES = 2 * 128 * 2048 * 4 + 2 * 16 * 2048 + 2048 * 4 + 2 * 128 * 128 * 4 + 2 * 16 * 128 + 128 * 32 * 2 + 128 * 128 * 4
@@ -57,7 +58,8 @@ def tile_attend_rel2_cap_srtq128n512t2048_kernel(tc, q_words, q_scales, k_words,
         zero = sb.tile([P, 1], F32, name="zero")
         nc.gpsimd.memset(zero[:], 0.0)
         nc.vector.memset(ks_pool[0:KS_ROW, :].bitcast(I32), 0)
-        nc.vector.memset(vs_pool[0:VS_ROW, :].bitcast(I32), 0)
+        nc.gpsimd.memset(vs_pool[0:VS_ROW, 0:FILL_SHARE].bitcast(I32), 0)
+        nc.vector.memset(vs_pool[0:VS_ROW, FILL_SHARE:].bitcast(I32), 0)
         nc.vector.memset(planes[:].bitcast(I32), 0)
 
         nc.sync.dma_start(offsets[:], offs)

@@ -6,13 +6,14 @@ T = 2048
 N = 512
 PASSES = 2
 PACK = 4
-RUN = 8
 CAP = 2.0
 VS_ROW = 127
 KS_ROW = 96
-V_FIRST = 960
-HALF = N // 2
-V_HALF = T - N + HALF
+V_FIRST = 704
+BLOCK = 32
+SHARE = 256
+PREFIX = T - N + SHARE
+TAIL = 128
 ROW = 640
 FILL_SHARE = 896
 
@@ -31,12 +32,8 @@ ACT = mybir.ActivationFunctionType
 ALU = mybir.AluOpType
 
 
-def by_place(rows, run):
-    return rows.rearrange("p (j t r) -> p t j r", t=PACK, r=run)
-
-
-def places(tile, run):
-    return tile.rearrange("p (t j r) -> p t j r", t=PACK, r=run)
+def crossed(run, size):
+    return run.rearrange("p (b a x) -> p a b x", a=2, x=size)
 
 
 def tile_attend_rel2_cap_srtq128n512t2048_kernel(tc, q_words, q_scales, k_words, k_scales, vT, vs, offs, out):
@@ -55,8 +52,11 @@ def tile_attend_rel2_cap_srtq128n512t2048_kernel(tc, q_words, q_scales, k_words,
         planes = sb.tile([P, PASSES, ROW], U8, name="planes", align_bytes=64)
         ident = sb.tile([P, P], F32, name="ident", align_bytes=64)
 
+        v_rows = sb.tile([P, N], BF16, name="v_rows", align_bytes=64)
         zero = sb.tile([P, 1], F32, name="zero")
         nc.gpsimd.memset(zero[:], 0.0)
+        no_bias = v_rows[:].bitcast(F32)[:, N // 2 - 1 :]
+        nc.gpsimd.memset(no_bias, 0.0)
         nc.vector.memset(ks_pool[0:KS_ROW, :].bitcast(I32), 0)
         nc.gpsimd.memset(vs_pool[0:VS_ROW, 0:FILL_SHARE].bitcast(I32), 0)
         nc.vector.memset(vs_pool[0:VS_ROW, FILL_SHARE:].bitcast(I32), 0)
@@ -67,53 +67,58 @@ def tile_attend_rel2_cap_srtq128n512t2048_kernel(tc, q_words, q_scales, k_words,
         nc.sync.dma_start(vs_pool[VS_ROW:, :], vs[0:1, :])
         nc.scalar.dma_start(staged[KS_ROW:, N : N + P].bitcast(I32), q_scales[0].rearrange("o f q -> f o q").bitcast(I32))
         kw_words = k_words[0].rearrange("g t b -> g (t b)").bitcast(I32)
-        nc.sync.dma_start(kw_pool[:, 0:V_HALF], kw_words[:, 0:V_HALF])
-        nc.sync.dma_start(kw_pool[:, V_HALF:], kw_words[:, V_HALF:])
+        nc.sync.dma_start(kw_pool[:, 0:PREFIX], kw_words[:, 0:PREFIX])
+        nc.sync.dma_start(kw_pool[:, PREFIX:], kw_words[:, PREFIX:])
         nc.sync.dma_start(q_codes[:], q_words[0].rearrange("o g q r -> g o (q r)").bitcast(I32))
         nc.sync.dma_start(v_pool[:, 0:V_FIRST], vT[:, 0:V_FIRST])
         nc.scalar.activation(ident[:], zero[:].to_broadcast([P, P]), ACT.Copy)
         make_identity(nc, ident[:], nomemset=True)
 
-        ks_rows = []
-        for h, tag in enumerate(("gathered", "second")):
-            rows = sb.tile([P, HALF], U8, name=f"ks_rows{h}", tag=tag, align_bytes=64)
-            nc.vector.tensor_copy(rows[:], ks_pool[:].indirect(offsets[:, h * HALF // 16 : (h + 1) * HALF // 16]))
-            ks_rows.append(rows)
-        for h in range(2):
-            nc.vector.tensor_copy(
-                places(staged[:, 0:N].bitcast(I32), RUN // 4)[:, :, 8 * h : 8 * h + 8], by_place(ks_rows[h][:].bitcast(I32), RUN // 4)
-            )
+        ks_rows = sb.tile([P, N], U8, name="ks_rows", tag="gathered", align_bytes=64)
+        nc.vector.tensor_copy(ks_rows[:].rearrange("p (t s) -> p s t", t=PACK), ks_pool[:].indirect(offsets[:]))
+        ks_from = ks_rows[:].bitcast(I32).rearrange("p (t w) -> p t w", t=PACK)
+        ks_to = staged[:, 0:N].bitcast(I32).rearrange("p (t w) -> p t w", t=PACK)
+        nc.vector.tensor_copy(
+            ks_to[:, :, 0 : SHARE // 16].rearrange("p t (b a x) -> p t a b x", a=2, x=2),
+            ks_from[:, :, 0 : SHARE // 16].rearrange("p t (a b x) -> p t a b x", a=2, x=2),
+        )
+        nc.vector.tensor_copy(ks_to[:, :, SHARE // 16 :], ks_from[:, :, SHARE // 16 :])
         for quad in (0, 2, 1, 3):
             nc.sync.dma_start(
                 planes[32 * quad : 32 * quad + 4, :, :].bitcast(I32),
                 staged[KS_ROW + 8 * quad : KS_ROW + 8 * quad + 8, :].bitcast(I32),
             )
-        nc.sync.dma_start(v_pool[:, V_FIRST:V_HALF], vT[:, V_FIRST:V_HALF])
-        nc.sync.dma_start(v_pool[:, V_HALF:], vT[:, V_HALF:])
+        nc.sync.dma_start(v_pool[:, V_FIRST:PREFIX], vT[:, V_FIRST:PREFIX])
+        nc.sync.dma_start(v_pool[:, PREFIX:], vT[:, PREFIX:])
 
         vs_rows = sb.tile([P, N], F32, name="vs_rows", align_bytes=64)
         nc.scalar.activation(vs_rows[:], vs_pool[:].indirect(offsets[:]), ACT.Copy)
-        vs_placed = sb.tile([P, N], F32, name="vs_placed", align_bytes=64)
-        for u in range(2):
-            nc.scalar.activation(places(vs_placed[:], RUN)[:, 2 * u : 2 * u + 2], by_place(vs_rows[:], RUN)[:, 2 * u : 2 * u + 2], ACT.Copy)
+        vs_placed = sb.tile([P, PACK, P], F32, name="vs_placed", align_bytes=64)
+        nc.scalar.copy(
+            vs_placed[:, :, 0 : SHARE // PACK].rearrange("p t (b a r) -> p a b r t", a=2, r=BLOCK // PACK),
+            vs_rows[:, 0:SHARE].rearrange("p (a b r t) -> p a b r t", a=2, r=BLOCK // PACK, t=PACK),
+        )
+        nc.scalar.copy(
+            vs_placed[:, :, SHARE // PACK :].rearrange("p t s -> p s t"), vs_rows[:, SHARE:].rearrange("p (s t) -> p s t", t=PACK)
+        )
         vs_ps = ps.tile([P, PACK, P], F32, name="vs_ps")
         for t in range(PACK):
-            nc.tensor.transpose(vs_ps[:, t, :], vs_placed[:, t * P : (t + 1) * P], ident[:])
+            nc.tensor.transpose(vs_ps[:, t, :], vs_placed[:, t, :], ident[:])
         vs_slot = sb.tile([P, 1, PACK], F32, name="vs_slot")
         nc.scalar.activation(vs_slot[:, 0, :], vs_ps[:, :, VS_ROW], ACT.Copy, scale=CAP * CAP)
 
         k_pairs = sb.tile([P, N], U32, name="k_pairs", tag="gathered", align_bytes=64)
-        nc.vector.tensor_copy(k_pairs[:, 0:HALF], kw_pool[:, 0:V_HALF].bitcast(U32).indirect(offsets[:, 0 : HALF // 16]))
-        nc.vector.tensor_copy(k_pairs[:, HALF:], kw_pool[:].bitcast(U32).indirect(offsets[:, HALF // 16 :]))
-        halves = k_pairs[:].bitcast(U16).rearrange("p (j t r o) -> p t o j r", t=PACK, r=RUN, o=PASSES)
+        nc.vector.tensor_copy(crossed(k_pairs[:, 0:SHARE], BLOCK), kw_pool[:, 0:PREFIX].bitcast(U32).indirect(offsets[:, 0 : SHARE // 16]))
+        nc.vector.tensor_copy(k_pairs[:, SHARE:], kw_pool[:].bitcast(U32).indirect(offsets[:, SHARE // 16 :]))
+        halves = k_pairs[:].bitcast(U16).rearrange("p (s t o) -> p t s o", t=PACK, o=PASSES)
         query_halves = (slice(0, P // 2), slice(P // 2, P))
-        th = sb.tile([P, 2, P, 2], F32, name="th", align_bytes=64)
+        banks = []
         for u in range(2):
             scores = ps.tile([P, 2, P], F32, name=f"scores{u}", tag=f"bank{u}")
             for e in range(2):
                 t = 2 * u + e
                 k_codes = sb.tile([P, PASSES, 2 * P], U8, name=f"k_codes{t}", align_bytes=64)
-                nc.vector.tensor_copy(k_codes[:].bitcast(U16).rearrange("p o (j r) -> p o j r", r=RUN), halves[:, t])
+                nc.vector.tensor_copy(k_codes[:].bitcast(U16).rearrange("p o s -> p s o"), halves[:, t])
                 for o in range(PASSES):
                     nc.tensor.matmul_mx(
                         out=scores[:, e, :],
@@ -124,24 +129,32 @@ def tile_attend_rel2_cap_srtq128n512t2048_kernel(tc, q_words, q_scales, k_words,
                         start=(o == 0),
                         stop=(o == PASSES - 1),
                     )
-            for qs in query_halves:
-                nc.scalar.activation(th[:, u, qs, :], scores[:, :, qs].rearrange("p e q -> p q e"), ACT.Tanh, scale=1.0 / CAP)
+            banks.append(scores)
 
-        v_rows = sb.tile([P, 2, N // 2], BF16, name="v_rows", align_bytes=64)
-        v_blocks = v_rows[:].rearrange("p u (j r e) -> p j u e r", r=RUN, e=2)
-        nc.vector.tensor_copy(v_blocks[:, 0:8], v_pool[:, 0:V_HALF].indirect(offsets[:, 0 : HALF // 16]))
-        nc.vector.tensor_copy(v_blocks[:, 8:16], v_pool[:].indirect(offsets[:, HALF // 16 :]))
+        def capped(th, scores, biases):
+            for qs, bias in zip(query_halves, biases):
+                nc.scalar.activation(th[:, qs, :], scores[:, :, qs].rearrange("p e q -> p q e"), ACT.Tanh, bias=bias, scale=1.0 / CAP)
+
+        th_first = sb.tile([P, P, 2], F32, name="th_first", align_bytes=64)
+        capped(th_first, banks[0], (no_bias, zero[:]))
+
+        nc.vector.tensor_copy(crossed(v_rows[:, 0:SHARE], BLOCK), v_pool[:, 0:PREFIX].indirect(offsets[:, 0 : SHARE // 16]))
+        nc.vector.tensor_copy(v_rows[:, SHARE : N - TAIL], v_pool[:].indirect(offsets[:, SHARE // 16 : (N - TAIL) // 16]))
+        nc.scalar.activation(v_rows[:, N - TAIL :], v_pool[:].indirect(offsets[:, (N - TAIL) // 16 :]), ACT.Copy)
+        late = sb.tile([P, 3, P, 2], F32, name="late", tag="values", align_bytes=64)
+        capped(late[:, 2], banks[1], (zero[:], zero[:]))
+        th = (th_first, late[:, 2])
         v_ps = ps.tile([P, 2, P], F32, name="v_ps", tag="bank0")
         for u in range(2):
-            nc.tensor.transpose(v_ps[:, u, :], v_rows[:, u, :].bitcast(F32), ident[:])
-        v_bf = sb.tile([P, P * PACK], BF16, name="v_bf", align_bytes=64)
+            nc.tensor.transpose(v_ps[:, u, :], v_rows[:].bitcast(F32)[:, u::2], ident[:])
+        v_bf = sb.tile([P, P * PACK], BF16, name="v_bf", tag="turned", align_bytes=64)
         nc.scalar.copy(v_bf[:].bitcast(F32).rearrange("p (f u) -> p f u", u=2), v_ps[:].rearrange("p u f -> p f u"))
 
-        sq = sb.tile([P, 2, P, 2], F32, name="sq", tag="values", align_bytes=64)
+        sq = late[:, 0:2]
         for u, qs in ((0, slice(0, P)), (1, query_halves[0]), (1, query_halves[1])):
-            part = th[:, u, qs, :]
+            part = th[u][:, qs, :]
             nc.vector.scalar_tensor_tensor(sq[:, u, qs, :], part, 0.0, part, ALU.max, ALU.mult)
-        w_bf = sb.tile([P, P, 2, 2], BF16, name="w_bf", tag="weights", align_bytes=64)
+        w_bf = sb.tile([P, P, 2, 2], BF16, name="w_bf", align_bytes=64)
         for qs in query_halves:
             nc.vector.tensor_tensor(
                 w_bf[:, qs],
@@ -166,9 +179,9 @@ def tile_attend_rel2_cap_srtq128n512t2048_kernel(tc, q_words, q_scales, k_words,
         w_flat = w_bf[:].rearrange("p q u e -> p (q u e)")
         first, second = query_halves
         nc.vector.quantize_mx(out=w_codes[:, first].bitcast(FP8X4), scales=w_plane[:, first], in_=w_flat[:, 0 : N // 2])
-        nc.vector.quantize_mx(out=v_codes[:].bitcast(FP8X4), scales=v_plane[:], in_=v_bf[:])
         nc.vector.quantize_mx(out=w_codes[:, second].bitcast(FP8X4), scales=w_plane[:, second], in_=w_flat[:, N // 2 :])
-        inv = sb.tile([P, 1], F32, name="inv", tag="weights", align_bytes=64)
+        nc.vector.quantize_mx(out=v_codes[:].bitcast(FP8X4), scales=v_plane[:], in_=v_bf[:])
+        inv = sb.tile([P, 1], F32, name="inv", tag="turned", align_bytes=64)
         nc.vector.reciprocal(inv[:], total[:])
 
         y_ps = ps.tile([P, P], F32, name="y_ps")

@@ -15,7 +15,6 @@ SHARE = 256
 PREFIX = T - N + SHARE
 TAIL = 128
 ROW = 640
-FILL_SHARE = 896
 
 FLOPS = 2 * 128 * 512 * 1024 + 2 * 128 * 512 * 128
 BYTES = 2 * 128 * 2048 * 4 + 2 * 16 * 2048 + 2048 * 4 + 2 * 128 * 128 * 4 + 2 * 16 * 128 + 128 * 32 * 2 + 128 * 128 * 4
@@ -43,11 +42,11 @@ def tile_attend_rel2_cap_srtq128n512t2048_kernel(tc, q_words, q_scales, k_words,
         tc.psum_pool(name="ps", bufs=1) as ps,
     ):
         offsets = sb.tile([P, N // 16], U16, name="offsets")
-        ks_pool = sb.tile([P, T], U8, name="ks_pool", align_bytes=64)
-        kw_pool = sb.tile([P, T], I32, name="kw_pool", align_bytes=64)
-        v_pool = sb.tile([P, T], F32, name="v_pool", tag="values", align_bytes=64)
-        vs_pool = sb.tile([P, T], F32, name="vs_pool", align_bytes=64)
-        q_codes = sb.tile([P, PASSES, P], I32, name="q_codes", align_bytes=64)
+        ks_pool = sb.tile([P, T], U8, name="ks_pool", align_bytes=256)
+        kw_pool = sb.tile([P, T], I32, name="kw_pool", align_bytes=256)
+        v_pool = sb.tile([P, T], F32, name="v_pool", tag="values", align_bytes=256)
+        vs_pool = sb.tile([P, T], F32, name="vs_pool", align_bytes=256)
+        q_codes = sb.tile([P, PASSES, P], I32, name="q_codes", align_bytes=256)
         staged = sb.tile([P, ROW], U8, name="staged", align_bytes=64)
         planes = sb.tile([P, PASSES, ROW], U8, name="planes", align_bytes=64)
         ident = sb.tile([P, P], F32, name="ident", align_bytes=64)
@@ -58,8 +57,7 @@ def tile_attend_rel2_cap_srtq128n512t2048_kernel(tc, q_words, q_scales, k_words,
         no_bias = v_rows[:].bitcast(F32)[:, N // 2 - 1 :]
         nc.gpsimd.memset(no_bias, 0.0)
         nc.vector.memset(ks_pool[0:KS_ROW, :].bitcast(I32), 0)
-        nc.gpsimd.memset(vs_pool[0:VS_ROW, 0:FILL_SHARE].bitcast(I32), 0)
-        nc.vector.memset(vs_pool[0:VS_ROW, FILL_SHARE:].bitcast(I32), 0)
+        nc.vector.memset(vs_pool[0:VS_ROW, :].bitcast(I32), 0)
         nc.vector.memset(planes[:].bitcast(I32), 0)
 
         nc.sync.dma_start(offsets[:], offs)
@@ -141,7 +139,7 @@ def tile_attend_rel2_cap_srtq128n512t2048_kernel(tc, q_words, q_scales, k_words,
         nc.vector.tensor_copy(crossed(v_rows[:, 0:SHARE], BLOCK), v_pool[:, 0:PREFIX].indirect(offsets[:, 0 : SHARE // 16]))
         nc.vector.tensor_copy(v_rows[:, SHARE : N - TAIL], v_pool[:].indirect(offsets[:, SHARE // 16 : (N - TAIL) // 16]))
         nc.scalar.activation(v_rows[:, N - TAIL :], v_pool[:].indirect(offsets[:, (N - TAIL) // 16 :]), ACT.Copy)
-        late = sb.tile([P, 3, P, 2], F32, name="late", tag="values", align_bytes=64)
+        late = sb.tile([P, 3, P, 2], F32, name="late", tag="values", align_bytes=256)
         capped(late[:, 2], banks[1], (zero[:], zero[:]))
         th = (th_first, late[:, 2])
         v_ps = ps.tile([P, 2, P], F32, name="v_ps", tag="bank0")
@@ -194,6 +192,6 @@ def tile_attend_rel2_cap_srtq128n512t2048_kernel(tc, q_words, q_scales, k_words,
             start=True,
             stop=True,
         )
-        y = sb.tile([P, P], F32, name="y")
+        y = sb.tile([P, P], F32, name="y", align_bytes=256)
         nc.vector.tensor_scalar(y[:], y_ps[:], inv[:], None, ALU.mult)
         nc.sync.dma_start(out[0], y[:])

@@ -9,11 +9,10 @@ PACK = 4
 CAP = 2.0
 VS_ROW = 127
 KS_ROW = 96
-V_FIRST = 704
-BLOCK = 32
+V_FIRST = 576
+GROUP = 128
 SHARE = 256
 PREFIX = T - N + SHARE
-TAIL = 128
 ROW = 640
 
 FLOPS = 2 * 128 * 512 * 1024 + 2 * 128 * 512 * 128
@@ -31,8 +30,8 @@ ACT = mybir.ActivationFunctionType
 ALU = mybir.AluOpType
 
 
-def crossed(run, size):
-    return run.rearrange("p (b a x) -> p a b x", a=2, x=size)
+def by_half(row):
+    return row.rearrange("p (g h x) -> p h g x", g=2, h=2)
 
 
 def tile_attend_rel2_cap_srtq128n512t2048_kernel(tc, q_words, q_scales, k_words, k_scales, vT, vs, offs, out):
@@ -47,8 +46,8 @@ def tile_attend_rel2_cap_srtq128n512t2048_kernel(tc, q_words, q_scales, k_words,
         v_pool = sb.tile([P, T], F32, name="v_pool", tag="values", align_bytes=256)
         vs_pool = sb.tile([P, T], F32, name="vs_pool", align_bytes=256)
         q_codes = sb.tile([P, PASSES, P], I32, name="q_codes", align_bytes=256)
-        staged = sb.tile([P, ROW], U8, name="staged", align_bytes=64)
-        planes = sb.tile([P, PASSES, ROW], U8, name="planes", align_bytes=64)
+        staged = sb.tile([P, ROW], U8, name="staged", align_bytes=256)
+        planes = sb.tile([P, PASSES, ROW], U8, name="planes", align_bytes=256)
         ident = sb.tile([P, P], F32, name="ident", align_bytes=64)
 
         v_rows = sb.tile([P, N], BF16, name="v_rows", align_bytes=64)
@@ -73,14 +72,8 @@ def tile_attend_rel2_cap_srtq128n512t2048_kernel(tc, q_words, q_scales, k_words,
         make_identity(nc, ident[:], nomemset=True)
 
         ks_rows = sb.tile([P, N], U8, name="ks_rows", tag="gathered", align_bytes=64)
-        nc.vector.tensor_copy(ks_rows[:].rearrange("p (t s) -> p s t", t=PACK), ks_pool[:].indirect(offsets[:]))
-        ks_from = ks_rows[:].bitcast(I32).rearrange("p (t w) -> p t w", t=PACK)
-        ks_to = staged[:, 0:N].bitcast(I32).rearrange("p (t w) -> p t w", t=PACK)
-        nc.vector.tensor_copy(
-            ks_to[:, :, 0 : SHARE // 16].rearrange("p t (b a x) -> p t a b x", a=2, x=2),
-            ks_from[:, :, 0 : SHARE // 16].rearrange("p t (a b x) -> p t a b x", a=2, x=2),
-        )
-        nc.vector.tensor_copy(ks_to[:, :, SHARE // 16 :], ks_from[:, :, SHARE // 16 :])
+        nc.vector.tensor_copy(ks_rows[:].rearrange("p (t g h s) -> p h g s t", t=PACK, g=2, h=2), ks_pool[:].indirect(offsets[:]))
+        nc.vector.tensor_copy(staged[:, 0:N].bitcast(I32), ks_rows[:].bitcast(I32))
         for quad in (0, 2, 1, 3):
             nc.sync.dma_start(
                 planes[32 * quad : 32 * quad + 4, :, :].bitcast(I32),
@@ -92,13 +85,11 @@ def tile_attend_rel2_cap_srtq128n512t2048_kernel(tc, q_words, q_scales, k_words,
         vs_rows = sb.tile([P, N], F32, name="vs_rows", align_bytes=64)
         nc.scalar.activation(vs_rows[:], vs_pool[:].indirect(offsets[:]), ACT.Copy)
         vs_placed = sb.tile([P, PACK, P], F32, name="vs_placed", align_bytes=64)
-        nc.scalar.copy(
-            vs_placed[:, :, 0 : SHARE // PACK].rearrange("p t (b a r) -> p a b r t", a=2, r=BLOCK // PACK),
-            vs_rows[:, 0:SHARE].rearrange("p (a b r t) -> p a b r t", a=2, r=BLOCK // PACK, t=PACK),
-        )
-        nc.scalar.copy(
-            vs_placed[:, :, SHARE // PACK :].rearrange("p t s -> p s t"), vs_rows[:, SHARE:].rearrange("p (s t) -> p s t", t=PACK)
-        )
+        for h in range(2):
+            nc.scalar.copy(
+                vs_placed[:].rearrange("p t (g h s) -> p h g s t", g=2, h=2)[:, h],
+                vs_rows[:].rearrange("p (h g s t) -> p h g s t", h=2, g=2, t=PACK)[:, h],
+            )
         vs_ps = ps.tile([P, PACK, P], F32, name="vs_ps")
         for t in range(PACK):
             nc.tensor.transpose(vs_ps[:, t, :], vs_placed[:, t, :], ident[:])
@@ -106,8 +97,8 @@ def tile_attend_rel2_cap_srtq128n512t2048_kernel(tc, q_words, q_scales, k_words,
         nc.scalar.activation(vs_slot[:, 0, :], vs_ps[:, :, VS_ROW], ACT.Copy, scale=CAP * CAP)
 
         k_pairs = sb.tile([P, N], U32, name="k_pairs", tag="gathered", align_bytes=64)
-        nc.vector.tensor_copy(crossed(k_pairs[:, 0:SHARE], BLOCK), kw_pool[:, 0:PREFIX].bitcast(U32).indirect(offsets[:, 0 : SHARE // 16]))
-        nc.vector.tensor_copy(k_pairs[:, SHARE:], kw_pool[:].bitcast(U32).indirect(offsets[:, SHARE // 16 :]))
+        nc.vector.tensor_copy(by_half(k_pairs[:])[:, 0], kw_pool[:, 0:PREFIX].bitcast(U32).indirect(offsets[:, 0 : SHARE // 16]))
+        nc.vector.tensor_copy(by_half(k_pairs[:])[:, 1], kw_pool[:].bitcast(U32).indirect(offsets[:, SHARE // 16 :]))
         halves = k_pairs[:].bitcast(U16).rearrange("p (s t o) -> p t s o", t=PACK, o=PASSES)
         query_halves = (slice(0, P // 2), slice(P // 2, P))
         banks = []
@@ -136,9 +127,9 @@ def tile_attend_rel2_cap_srtq128n512t2048_kernel(tc, q_words, q_scales, k_words,
         th_first = sb.tile([P, P, 2], F32, name="th_first", align_bytes=64)
         capped(th_first, banks[0], (no_bias, zero[:]))
 
-        nc.vector.tensor_copy(crossed(v_rows[:, 0:SHARE], BLOCK), v_pool[:, 0:PREFIX].indirect(offsets[:, 0 : SHARE // 16]))
-        nc.vector.tensor_copy(v_rows[:, SHARE : N - TAIL], v_pool[:].indirect(offsets[:, SHARE // 16 : (N - TAIL) // 16]))
-        nc.scalar.activation(v_rows[:, N - TAIL :], v_pool[:].indirect(offsets[:, (N - TAIL) // 16 :]), ACT.Copy)
+        nc.vector.tensor_copy(by_half(v_rows[:])[:, 0], v_pool[:, 0:PREFIX].indirect(offsets[:, 0 : SHARE // 16]))
+        nc.vector.tensor_copy(by_half(v_rows[:])[:, 1, 0], v_pool[:].indirect(offsets[:, SHARE // 16 : (N - GROUP) // 16]))
+        nc.scalar.activation(by_half(v_rows[:])[:, 1, 1], v_pool[:].indirect(offsets[:, (N - GROUP) // 16 :]), ACT.Copy)
         late = sb.tile([P, 3, P, 2], F32, name="late", tag="values", align_bytes=256)
         capped(late[:, 2], banks[1], (zero[:], zero[:]))
         th = (th_first, late[:, 2])
@@ -177,8 +168,8 @@ def tile_attend_rel2_cap_srtq128n512t2048_kernel(tc, q_words, q_scales, k_words,
         w_flat = w_bf[:].rearrange("p q u e -> p (q u e)")
         first, second = query_halves
         nc.vector.quantize_mx(out=w_codes[:, first].bitcast(FP8X4), scales=w_plane[:, first], in_=w_flat[:, 0 : N // 2])
-        nc.vector.quantize_mx(out=w_codes[:, second].bitcast(FP8X4), scales=w_plane[:, second], in_=w_flat[:, N // 2 :])
         nc.vector.quantize_mx(out=v_codes[:].bitcast(FP8X4), scales=v_plane[:], in_=v_bf[:])
+        nc.vector.quantize_mx(out=w_codes[:, second].bitcast(FP8X4), scales=w_plane[:, second], in_=w_flat[:, N // 2 :])
         inv = sb.tile([P, 1], F32, name="inv", tag="turned", align_bytes=64)
         nc.vector.reciprocal(inv[:], total[:])
 

@@ -9,7 +9,7 @@ PACK = 4
 CAP = 2.0
 VS_ROW = 127
 KS_ROW = 96
-V_FIRST = 576
+V_FIRST = 640
 GROUP = 128
 SHARE = 256
 PREFIX = T - N + SHARE
@@ -41,13 +41,12 @@ def tile_attend_rel2_cap_srtq128n512t2048_kernel(tc, q_words, q_scales, k_words,
         tc.psum_pool(name="ps", bufs=1) as ps,
     ):
         offsets = sb.tile([P, N // 16], U16, name="offsets")
-        ks_pool = sb.tile([P, T], U8, name="ks_pool", align_bytes=256)
+        ks_pool = sb.tile([P, T], U8, name="ks_pool", tag="scales", align_bytes=256)
         kw_pool = sb.tile([P, T], I32, name="kw_pool", align_bytes=256)
         v_pool = sb.tile([P, T], F32, name="v_pool", tag="values", align_bytes=256)
         vs_pool = sb.tile([P, T], F32, name="vs_pool", align_bytes=256)
         q_codes = sb.tile([P, PASSES, P], I32, name="q_codes", align_bytes=256)
         staged = sb.tile([P, ROW], U8, name="staged", align_bytes=256)
-        planes = sb.tile([P, PASSES, ROW], U8, name="planes", align_bytes=256)
         ident = sb.tile([P, P], F32, name="ident", align_bytes=64)
 
         v_rows = sb.tile([P, N], BF16, name="v_rows", align_bytes=64)
@@ -57,7 +56,6 @@ def tile_attend_rel2_cap_srtq128n512t2048_kernel(tc, q_words, q_scales, k_words,
         nc.gpsimd.memset(no_bias, 0.0)
         nc.vector.memset(ks_pool[0:KS_ROW, :].bitcast(I32), 0)
         nc.vector.memset(vs_pool[0:VS_ROW, :].bitcast(I32), 0)
-        nc.vector.memset(planes[:].bitcast(I32), 0)
 
         nc.sync.dma_start(offsets[:], offs)
         nc.scalar.dma_start(ks_pool[KS_ROW:, :].bitcast(I32), k_scales.rearrange("o f t -> f o t").bitcast(I32))
@@ -74,6 +72,7 @@ def tile_attend_rel2_cap_srtq128n512t2048_kernel(tc, q_words, q_scales, k_words,
         ks_rows = sb.tile([P, N], U8, name="ks_rows", tag="gathered", align_bytes=64)
         nc.vector.tensor_copy(ks_rows[:].rearrange("p (t g h s) -> p h g s t", t=PACK, g=2, h=2), ks_pool[:].indirect(offsets[:]))
         nc.vector.tensor_copy(staged[:, 0:N].bitcast(I32), ks_rows[:].bitcast(I32))
+        planes = sb.tile([P, PASSES, ROW], U8, name="planes", tag="scales", align_bytes=256)
         for quad in (0, 2, 1, 3):
             nc.sync.dma_start(
                 planes[32 * quad : 32 * quad + 4, :, :].bitcast(I32),

@@ -9,7 +9,7 @@ PACK = 4
 CAP = 2.0
 VS_ROW = 127
 KS_ROW = 96
-V_FIRST = 640
+V_FIRST = 704
 GROUP = 128
 SHARE = 256
 PREFIX = T - N + SHARE

@@ -101,60 +101,56 @@ def tile_attend_rel2_cap_srtq128n512t2048_kernel(tc, q_words, q_scales, k_words,
         halves = k_pairs[:].bitcast(U16).rearrange("p (s t o) -> p t s o", t=PACK, o=PASSES)
         query_halves = (slice(0, P // 2), slice(P // 2, P))
         banks = []
-        for u in range(2):
-            scores = ps.tile([P, 2, P], F32, name=f"scores{u}", tag=f"bank{u}")
-            for e in range(2):
-                t = 2 * u + e
-                k_codes = sb.tile([P, PASSES, 2 * P], U8, name=f"k_codes{t}", align_bytes=64)
-                nc.vector.tensor_copy(k_codes[:].bitcast(U16).rearrange("p o s -> p s o"), halves[:, t])
-                for o in range(PASSES):
-                    nc.tensor.matmul_mx(
-                        out=scores[:, e, :],
-                        lhsT=k_codes[:, o, :].bitcast(FP4X4),
-                        lhsT_scale=planes[:, o, t * P : (t + 1) * P],
-                        rhs=q_codes[:, o, :].bitcast(FP8X4),
-                        rhs_scale=planes[:, o, N : N + P],
-                        start=(o == 0),
-                        stop=(o == PASSES - 1),
-                    )
+        for t in range(PACK):
+            scores = ps.tile([P, P], F32, name=f"scores{t}", tag=f"bank{t}")
+            k_codes = sb.tile([P, PASSES, 2 * P], U8, name=f"k_codes{t}", align_bytes=64)
+            nc.vector.tensor_copy(k_codes[:].bitcast(U16).rearrange("p o s -> p s o"), halves[:, t])
+            for o in range(PASSES):
+                nc.tensor.matmul_mx(
+                    out=scores[:],
+                    lhsT=k_codes[:, o, :].bitcast(FP4X4),
+                    lhsT_scale=planes[:, o, t * P : (t + 1) * P],
+                    rhs=q_codes[:, o, :].bitcast(FP8X4),
+                    rhs_scale=planes[:, o, N : N + P],
+                    start=(o == 0),
+                    stop=(o == PASSES - 1),
+                )
             banks.append(scores)
 
-        def capped(th, scores, biases):
-            for qs, bias in zip(query_halves, biases):
-                nc.scalar.activation(th[:, qs, :], scores[:, :, qs].rearrange("p e q -> p q e"), ACT.Tanh, bias=bias, scale=1.0 / CAP)
+        def capped(th, t, bias):
+            nc.scalar.activation(th, banks[t][:], ACT.Tanh, bias=bias, scale=1.0 / CAP)
 
-        th_first = sb.tile([P, P, 2], F32, name="th_first", align_bytes=64)
-        capped(th_first, banks[0], (no_bias, zero[:]))
+        th_first = sb.tile([P, PACK - 1, P], F32, name="th_first", align_bytes=64)
+        for t, bias in enumerate((zero[:], zero[:], no_bias)):
+            capped(th_first[:, t], t, bias)
 
         nc.vector.tensor_copy(by_half(v_rows[:])[:, 0], v_pool[:, 0:PREFIX].indirect(offsets[:, 0 : SHARE // 16]))
         nc.vector.tensor_copy(by_half(v_rows[:])[:, 1, 0], v_pool[:].indirect(offsets[:, SHARE // 16 : (N - GROUP) // 16]))
         nc.scalar.activation(by_half(v_rows[:])[:, 1, 1], v_pool[:].indirect(offsets[:, (N - GROUP) // 16 :]), ACT.Copy)
-        late = sb.tile([P, 3, P, 2], F32, name="late", tag="values", align_bytes=256)
-        capped(late[:, 2], banks[1], (zero[:], zero[:]))
-        th = (th_first, late[:, 2])
+        late = sb.tile([P, PACK + 1, P], F32, name="late", tag="values", align_bytes=256)
+        capped(late[:, PACK], PACK - 1, zero[:])
         v_ps = ps.tile([P, 2, P], F32, name="v_ps", tag="bank0")
         for u in range(2):
             nc.tensor.transpose(v_ps[:, u, :], v_rows[:].bitcast(F32)[:, u::2], ident[:])
         v_bf = sb.tile([P, P * PACK], BF16, name="v_bf", tag="turned", align_bytes=64)
         nc.scalar.copy(v_bf[:].bitcast(F32).rearrange("p (f u) -> p f u", u=2), v_ps[:].rearrange("p u f -> p f u"))
 
-        sq = late[:, 0:2]
-        for u, qs in ((0, slice(0, P)), (1, query_halves[0]), (1, query_halves[1])):
-            part = th[u][:, qs, :]
-            nc.vector.scalar_tensor_tensor(sq[:, u, qs, :], part, 0.0, part, ALU.max, ALU.mult)
-        w_bf = sb.tile([P, P, 2, 2], BF16, name="w_bf", align_bytes=64)
+        sq = late[:, 0:PACK]
+        for places, part in ((slice(0, PACK - 1), th_first[:]), (slice(PACK - 1, PACK), late[:, PACK:])):
+            nc.vector.scalar_tensor_tensor(sq[:, places], part, 0.0, part, ALU.max, ALU.mult)
+        w_bf = sb.tile([P, P, PACK], BF16, name="w_bf", align_bytes=64)
         for qs in query_halves:
             nc.vector.tensor_tensor(
-                w_bf[:, qs],
-                sq[:, :, qs, :].rearrange("p u q e -> p q u e"),
-                vs_slot[:].rearrange("p one (u e) -> p one u e", e=2).to_broadcast([P, P // 2, 2, 2]),
+                w_bf[:, qs].rearrange("p (c i) t -> p c t i", i=4),
+                sq[:, :, qs].rearrange("p t (c i) -> p c t i", i=4),
+                vs_slot[:].rearrange("p one (t i) -> p one t i", i=1).to_broadcast([P, P // 8, PACK, 4]),
                 ALU.mult,
             )
 
         l_ps = ps.tile([P, P], F32, name="l_ps")
         for t in range(PACK):
             nc.tensor.matmul(
-                l_ps[:], lhsT=sq[:, t // 2, :, t % 2], rhs=ident[:], is_transpose=True, start=(t == 0), stop=(t == PACK - 1)
+                l_ps[:], lhsT=sq[:, t, :], rhs=ident[:], is_transpose=True, start=(t == 0), stop=(t == PACK - 1)
             )
         l_terms = sb.tile([P, P], F32, name="l_terms")
         total = sb.tile([P, 1], F32, name="total")
@@ -164,7 +160,7 @@ def tile_attend_rel2_cap_srtq128n512t2048_kernel(tc, q_words, q_scales, k_words,
         w_plane = sb.tile([P, P], U8, name="w_plane", align_bytes=64)
         v_codes = sb.tile([P, P], U32, name="v_codes", align_bytes=64)
         v_plane = sb.tile([P, P], U8, name="v_plane", align_bytes=64)
-        w_flat = w_bf[:].rearrange("p q u e -> p (q u e)")
+        w_flat = w_bf[:].rearrange("p q t -> p (q t)")
         first, second = query_halves
         nc.vector.quantize_mx(out=w_codes[:, first].bitcast(FP8X4), scales=w_plane[:, first], in_=w_flat[:, 0 : N // 2])
         nc.vector.quantize_mx(out=v_codes[:].bitcast(FP8X4), scales=v_plane[:], in_=v_bf[:])

@@ -101,56 +101,61 @@ def tile_attend_rel2_cap_srtq128n512t2048_kernel(tc, q_words, q_scales, k_words,
         halves = k_pairs[:].bitcast(U16).rearrange("p (s t o) -> p t s o", t=PACK, o=PASSES)
         query_halves = (slice(0, P // 2), slice(P // 2, P))
         banks = []
-        for t in range(PACK):
-            scores = ps.tile([P, P], F32, name=f"scores{t}", tag=f"bank{t}")
-            k_codes = sb.tile([P, PASSES, 2 * P], U8, name=f"k_codes{t}", align_bytes=64)
-            nc.vector.tensor_copy(k_codes[:].bitcast(U16).rearrange("p o s -> p s o"), halves[:, t])
-            for o in range(PASSES):
-                nc.tensor.matmul_mx(
-                    out=scores[:],
-                    lhsT=k_codes[:, o, :].bitcast(FP4X4),
-                    lhsT_scale=planes[:, o, t * P : (t + 1) * P],
-                    rhs=q_codes[:, o, :].bitcast(FP8X4),
-                    rhs_scale=planes[:, o, N : N + P],
-                    start=(o == 0),
-                    stop=(o == PASSES - 1),
-                )
-            banks.append(scores)
+        for u in range(2):
+            if u == 1:
+                pair = ps.tile([P, 2, P], F32, name="scores_pair")
+            for e in range(2):
+                t = 2 * u + e
+                if u == 0:
+                    scores = ps.tile([P, P], F32, name=f"scores{t}", tag=f"bank{t}")
+                    banks.append(scores)
+                k_codes = sb.tile([P, PASSES, 2 * P], U8, name=f"k_codes{t}", align_bytes=64)
+                nc.vector.tensor_copy(k_codes[:].bitcast(U16).rearrange("p o s -> p s o"), halves[:, t])
+                for o in range(PASSES):
+                    nc.tensor.matmul_mx(
+                        out=scores[:] if u == 0 else pair[:, e, :],
+                        lhsT=k_codes[:, o, :].bitcast(FP4X4),
+                        lhsT_scale=planes[:, o, t * P : (t + 1) * P],
+                        rhs=q_codes[:, o, :].bitcast(FP8X4),
+                        rhs_scale=planes[:, o, N : N + P],
+                        start=(o == 0),
+                        stop=(o == PASSES - 1),
+                    )
 
-        def capped(th, t, bias):
-            nc.scalar.activation(th, banks[t][:], ACT.Tanh, bias=bias, scale=1.0 / CAP)
-
-        th_first = sb.tile([P, PACK - 1, P], F32, name="th_first", align_bytes=64)
-        for t, bias in enumerate((zero[:], zero[:], no_bias)):
-            capped(th_first[:, t], t, bias)
+        th_first = sb.tile([P, 2, P], F32, name="th_first", align_bytes=64)
+        for e, bias in enumerate((no_bias, zero[:])):
+            nc.scalar.activation(th_first[:, e], banks[e][:], ACT.Tanh, bias=bias, scale=1.0 / CAP)
 
         nc.vector.tensor_copy(by_half(v_rows[:])[:, 0], v_pool[:, 0:PREFIX].indirect(offsets[:, 0 : SHARE // 16]))
         nc.vector.tensor_copy(by_half(v_rows[:])[:, 1, 0], v_pool[:].indirect(offsets[:, SHARE // 16 : (N - GROUP) // 16]))
         nc.scalar.activation(by_half(v_rows[:])[:, 1, 1], v_pool[:].indirect(offsets[:, (N - GROUP) // 16 :]), ACT.Copy)
-        late = sb.tile([P, PACK + 1, P], F32, name="late", tag="values", align_bytes=256)
-        capped(late[:, PACK], PACK - 1, zero[:])
+        late = sb.tile([P, 3, P, 2], F32, name="late", tag="values", align_bytes=256)
+        for qs in query_halves:
+            nc.scalar.activation(late[:, 2, qs, :], pair[:, :, qs].rearrange("p e q -> p q e"), ACT.Tanh, bias=zero[:], scale=1.0 / CAP)
+        th = (th_first[:].rearrange("p e q -> p q e"), late[:, 2])
         v_ps = ps.tile([P, 2, P], F32, name="v_ps", tag="bank0")
         for u in range(2):
             nc.tensor.transpose(v_ps[:, u, :], v_rows[:].bitcast(F32)[:, u::2], ident[:])
         v_bf = sb.tile([P, P * PACK], BF16, name="v_bf", tag="turned", align_bytes=64)
         nc.scalar.copy(v_bf[:].bitcast(F32).rearrange("p (f u) -> p f u", u=2), v_ps[:].rearrange("p u f -> p f u"))
 
-        sq = late[:, 0:PACK]
-        for places, part in ((slice(0, PACK - 1), th_first[:]), (slice(PACK - 1, PACK), late[:, PACK:])):
-            nc.vector.scalar_tensor_tensor(sq[:, places], part, 0.0, part, ALU.max, ALU.mult)
-        w_bf = sb.tile([P, P, PACK], BF16, name="w_bf", align_bytes=64)
+        sq = late[:, 0:2]
+        for u, qs in ((0, slice(0, P)), (1, query_halves[0]), (1, query_halves[1])):
+            part = th[u][:, qs, :]
+            nc.vector.scalar_tensor_tensor(sq[:, u, qs, :], part, 0.0, part, ALU.max, ALU.mult)
+        w_bf = sb.tile([P, P, 2, 2], BF16, name="w_bf", align_bytes=64)
         for qs in query_halves:
             nc.vector.tensor_tensor(
-                w_bf[:, qs].rearrange("p (c i) t -> p c t i", i=4),
-                sq[:, :, qs].rearrange("p t (c i) -> p c t i", i=4),
-                vs_slot[:].rearrange("p one (t i) -> p one t i", i=1).to_broadcast([P, P // 8, PACK, 4]),
+                w_bf[:, qs],
+                sq[:, :, qs, :].rearrange("p u q e -> p q u e"),
+                vs_slot[:].rearrange("p one (u e) -> p one u e", e=2).to_broadcast([P, P // 2, 2, 2]),
                 ALU.mult,
             )
 
         l_ps = ps.tile([P, P], F32, name="l_ps")
         for t in range(PACK):
             nc.tensor.matmul(
-                l_ps[:], lhsT=sq[:, t, :], rhs=ident[:], is_transpose=True, start=(t == 0), stop=(t == PACK - 1)
+                l_ps[:], lhsT=sq[:, t // 2, :, t % 2], rhs=ident[:], is_transpose=True, start=(t == 0), stop=(t == PACK - 1)
             )
         l_terms = sb.tile([P, P], F32, name="l_terms")
         total = sb.tile([P, 1], F32, name="total")
@@ -160,7 +165,7 @@ def tile_attend_rel2_cap_srtq128n512t2048_kernel(tc, q_words, q_scales, k_words,
         w_plane = sb.tile([P, P], U8, name="w_plane", align_bytes=64)
         v_codes = sb.tile([P, P], U32, name="v_codes", align_bytes=64)
         v_plane = sb.tile([P, P], U8, name="v_plane", align_bytes=64)
-        w_flat = w_bf[:].rearrange("p q t -> p (q t)")
+        w_flat = w_bf[:].rearrange("p q u e -> p (q u e)")
         first, second = query_halves
         nc.vector.quantize_mx(out=w_codes[:, first].bitcast(FP8X4), scales=w_plane[:, first], in_=w_flat[:, 0 : N // 2])
         nc.vector.quantize_mx(out=v_codes[:].bitcast(FP8X4), scales=v_plane[:], in_=v_bf[:])

@@ -61,10 +61,10 @@ def tile_attend_rel2_cap_srtq128n512t2048_kernel(tc, q_words, q_scales, k_words,
         nc.scalar.dma_start(ks_pool[KS_ROW:, :].bitcast(I32), k_scales.rearrange("o f t -> f o t").bitcast(I32))
         nc.sync.dma_start(vs_pool[VS_ROW:, :], vs[0:1, :])
         nc.scalar.dma_start(staged[KS_ROW:, N : N + P].bitcast(I32), q_scales[0].rearrange("o f q -> f o q").bitcast(I32))
+        nc.sync.dma_start(q_codes[:], q_words[0].rearrange("o g q r -> g o (q r)").bitcast(I32))
         kw_words = k_words[0].rearrange("g t b -> g (t b)").bitcast(I32)
         nc.sync.dma_start(kw_pool[:, 0:PREFIX], kw_words[:, 0:PREFIX])
         nc.sync.dma_start(kw_pool[:, PREFIX:], kw_words[:, PREFIX:])
-        nc.sync.dma_start(q_codes[:], q_words[0].rearrange("o g q r -> g o (q r)").bitcast(I32))
         nc.sync.dma_start(v_pool[:, 0:V_FIRST], vT[:, 0:V_FIRST])
         nc.scalar.activation(ident[:], zero[:].to_broadcast([P, P]), ACT.Copy)
         make_identity(nc, ident[:], nomemset=True)

@@ -9,7 +9,7 @@ PACK = 4
 CAP = 2.0
 VS_ROW = 127
 KS_ROW = 96
-V_FIRST = 704
+V_FIRST = 832
 GROUP = 128
 SHARE = 256
 PREFIX = T - N + SHARE

import concourse.mybir as mybir
from concourse.masks import make_identity

P = 128
T = 2048
N = 512
PASSES = 2
PACK = 4
CAP = 2.0
VS_ROW = 127
KS_ROW = 96
V_FIRST = 832
GROUP = 128
SHARE = 256
PREFIX = T - N + SHARE
ROW = 640

FLOPS = 2 * 128 * 512 * 1024 + 2 * 128 * 512 * 128
BYTES = 2 * 128 * 2048 * 4 + 2 * 16 * 2048 + 2048 * 4 + 2 * 128 * 128 * 4 + 2 * 16 * 128 + 128 * 32 * 2 + 128 * 128 * 4

F32 = mybir.dt.float32
BF16 = mybir.dt.bfloat16
I32 = mybir.dt.int32
U32 = mybir.dt.uint32
U16 = mybir.dt.uint16
U8 = mybir.dt.uint8
FP8X4 = mybir.dt.float8_e4m3fn_x4
FP4X4 = mybir.dt.float4_e2m1fn_x4
ACT = mybir.ActivationFunctionType
ALU = mybir.AluOpType


def by_half(row):
    return row.rearrange("p (g h x) -> p h g x", g=2, h=2)


def tile_attend_rel2_cap_srtq128n512t2048_kernel(tc, q_words, q_scales, k_words, k_scales, vT, vs, offs, out):
    nc = tc.nc
    with (
        tc.tile_pool(name="sb", bufs=1) as sb,
        tc.psum_pool(name="ps", bufs=1) as ps,
    ):
        offsets = sb.tile([P, N // 16], U16, name="offsets")
        ks_pool = sb.tile([P, T], U8, name="ks_pool", tag="scales", align_bytes=256)
        kw_pool = sb.tile([P, T], I32, name="kw_pool", align_bytes=256)
        v_pool = sb.tile([P, T], F32, name="v_pool", tag="values", align_bytes=256)
        vs_pool = sb.tile([P, T], F32, name="vs_pool", align_bytes=256)
        q_codes = sb.tile([P, PASSES, P], I32, name="q_codes", align_bytes=256)
        staged = sb.tile([P, ROW], U8, name="staged", align_bytes=256)
        ident = sb.tile([P, P], F32, name="ident", align_bytes=64)

        v_rows = sb.tile([P, N], BF16, name="v_rows", align_bytes=64)
        zero = sb.tile([P, 1], F32, name="zero")
        nc.gpsimd.memset(zero[:], 0.0)
        no_bias = v_rows[:].bitcast(F32)[:, N // 2 - 1 :]
        nc.gpsimd.memset(no_bias, 0.0)
        nc.vector.memset(ks_pool[0:KS_ROW, :].bitcast(I32), 0)
        nc.vector.memset(vs_pool[0:VS_ROW, :].bitcast(I32), 0)

        nc.sync.dma_start(offsets[:], offs)
        nc.scalar.dma_start(ks_pool[KS_ROW:, :].bitcast(I32), k_scales.rearrange("o f t -> f o t").bitcast(I32))
        nc.sync.dma_start(vs_pool[VS_ROW:, :], vs[0:1, :])
        nc.scalar.dma_start(staged[KS_ROW:, N : N + P].bitcast(I32), q_scales[0].rearrange("o f q -> f o q").bitcast(I32))
        nc.sync.dma_start(q_codes[:], q_words[0].rearrange("o g q r -> g o (q r)").bitcast(I32))
        kw_words = k_words[0].rearrange("g t b -> g (t b)").bitcast(I32)
        nc.sync.dma_start(kw_pool[:, 0:PREFIX], kw_words[:, 0:PREFIX])
        nc.sync.dma_start(kw_pool[:, PREFIX:], kw_words[:, PREFIX:])
        nc.sync.dma_start(v_pool[:, 0:V_FIRST], vT[:, 0:V_FIRST])
        nc.scalar.activation(ident[:], zero[:].to_broadcast([P, P]), ACT.Copy)
        make_identity(nc, ident[:], nomemset=True)

        ks_rows = sb.tile([P, N], U8, name="ks_rows", tag="gathered", align_bytes=64)
        nc.vector.tensor_copy(ks_rows[:].rearrange("p (t g h s) -> p h g s t", t=PACK, g=2, h=2), ks_pool[:].indirect(offsets[:]))
        nc.vector.tensor_copy(staged[:, 0:N].bitcast(I32), ks_rows[:].bitcast(I32))
        planes = sb.tile([P, PASSES, ROW], U8, name="planes", tag="scales", align_bytes=256)
        for quad in (0, 2, 1, 3):
            nc.sync.dma_start(
                planes[32 * quad : 32 * quad + 4, :, :].bitcast(I32),
                staged[KS_ROW + 8 * quad : KS_ROW + 8 * quad + 8, :].bitcast(I32),
            )
        nc.sync.dma_start(v_pool[:, V_FIRST:PREFIX], vT[:, V_FIRST:PREFIX])
        nc.sync.dma_start(v_pool[:, PREFIX:], vT[:, PREFIX:])

        vs_rows = sb.tile([P, N], F32, name="vs_rows", align_bytes=64)
        nc.scalar.activation(vs_rows[:], vs_pool[:].indirect(offsets[:]), ACT.Copy)
        vs_placed = sb.tile([P, PACK, P], F32, name="vs_placed", align_bytes=64)
        for h in range(2):
            nc.scalar.copy(
                vs_placed[:].rearrange("p t (g h s) -> p h g s t", g=2, h=2)[:, h],
                vs_rows[:].rearrange("p (h g s t) -> p h g s t", h=2, g=2, t=PACK)[:, h],
            )
        vs_ps = ps.tile([P, PACK, P], F32, name="vs_ps")
        for t in range(PACK):
            nc.tensor.transpose(vs_ps[:, t, :], vs_placed[:, t, :], ident[:])
        vs_slot = sb.tile([P, 1, PACK], F32, name="vs_slot")
        nc.scalar.activation(vs_slot[:, 0, :], vs_ps[:, :, VS_ROW], ACT.Copy, scale=CAP * CAP)

        k_pairs = sb.tile([P, N], U32, name="k_pairs", tag="gathered", align_bytes=64)
        nc.vector.tensor_copy(by_half(k_pairs[:])[:, 0], kw_pool[:, 0:PREFIX].bitcast(U32).indirect(offsets[:, 0 : SHARE // 16]))
        nc.vector.tensor_copy(by_half(k_pairs[:])[:, 1], kw_pool[:].bitcast(U32).indirect(offsets[:, SHARE // 16 :]))
        halves = k_pairs[:].bitcast(U16).rearrange("p (s t o) -> p t s o", t=PACK, o=PASSES)
        query_halves = (slice(0, P // 2), slice(P // 2, P))
        banks = []
        for u in range(2):
            if u == 1:
                pair = ps.tile([P, 2, P], F32, name="scores_pair")
            for e in range(2):
                t = 2 * u + e
                if u == 0:
                    scores = ps.tile([P, P], F32, name=f"scores{t}", tag=f"bank{t}")
                    banks.append(scores)
                k_codes = sb.tile([P, PASSES, 2 * P], U8, name=f"k_codes{t}", align_bytes=64)
                nc.vector.tensor_copy(k_codes[:].bitcast(U16).rearrange("p o s -> p s o"), halves[:, t])
                for o in range(PASSES):
                    nc.tensor.matmul_mx(
                        out=scores[:] if u == 0 else pair[:, e, :],
                        lhsT=k_codes[:, o, :].bitcast(FP4X4),
                        lhsT_scale=planes[:, o, t * P : (t + 1) * P],
                        rhs=q_codes[:, o, :].bitcast(FP8X4),
                        rhs_scale=planes[:, o, N : N + P],
                        start=(o == 0),
                        stop=(o == PASSES - 1),
                    )

        th_first = sb.tile([P, 2, P], F32, name="th_first", align_bytes=64)
        for e, bias in enumerate((no_bias, zero[:])):
            nc.scalar.activation(th_first[:, e], banks[e][:], ACT.Tanh, bias=bias, scale=1.0 / CAP)

        nc.vector.tensor_copy(by_half(v_rows[:])[:, 0], v_pool[:, 0:PREFIX].indirect(offsets[:, 0 : SHARE // 16]))
        nc.vector.tensor_copy(by_half(v_rows[:])[:, 1, 0], v_pool[:].indirect(offsets[:, SHARE // 16 : (N - GROUP) // 16]))
        nc.scalar.activation(by_half(v_rows[:])[:, 1, 1], v_pool[:].indirect(offsets[:, (N - GROUP) // 16 :]), ACT.Copy)
        late = sb.tile([P, 3, P, 2], F32, name="late", tag="values", align_bytes=256)
        for qs in query_halves:
            nc.scalar.activation(late[:, 2, qs, :], pair[:, :, qs].rearrange("p e q -> p q e"), ACT.Tanh, bias=zero[:], scale=1.0 / CAP)
        th = (th_first[:].rearrange("p e q -> p q e"), late[:, 2])
        v_ps = ps.tile([P, 2, P], F32, name="v_ps", tag="bank0")
        for u in range(2):
            nc.tensor.transpose(v_ps[:, u, :], v_rows[:].bitcast(F32)[:, u::2], ident[:])
        v_bf = sb.tile([P, P * PACK], BF16, name="v_bf", tag="turned", align_bytes=64)
        nc.scalar.copy(v_bf[:].bitcast(F32).rearrange("p (f u) -> p f u", u=2), v_ps[:].rearrange("p u f -> p f u"))

        sq = late[:, 0:2]
        for u, qs in ((0, slice(0, P)), (1, query_halves[0]), (1, query_halves[1])):
            part = th[u][:, qs, :]
            nc.vector.scalar_tensor_tensor(sq[:, u, qs, :], part, 0.0, part, ALU.max, ALU.mult)
        w_bf = sb.tile([P, P, 2, 2], BF16, name="w_bf", align_bytes=64)
        for qs in query_halves:
            nc.vector.tensor_tensor(
                w_bf[:, qs],
                sq[:, :, qs, :].rearrange("p u q e -> p q u e"),
                vs_slot[:].rearrange("p one (u e) -> p one u e", e=2).to_broadcast([P, P // 2, 2, 2]),
                ALU.mult,
            )

        l_ps = ps.tile([P, P], F32, name="l_ps")
        for t in range(PACK):
            nc.tensor.matmul(
                l_ps[:], lhsT=sq[:, t // 2, :, t % 2], rhs=ident[:], is_transpose=True, start=(t == 0), stop=(t == PACK - 1)
            )
        l_terms = sb.tile([P, P], F32, name="l_terms")
        total = sb.tile([P, 1], F32, name="total")
        nc.scalar.activation(l_terms[:], l_ps[:], ACT.Copy, scale=CAP * CAP, bias=1.0 / P, accum_out=total[:])

        w_codes = sb.tile([P, P], U32, name="w_codes", align_bytes=64)
        w_plane = sb.tile([P, P], U8, name="w_plane", align_bytes=64)
        v_codes = sb.tile([P, P], U32, name="v_codes", align_bytes=64)
        v_plane = sb.tile([P, P], U8, name="v_plane", align_bytes=64)
        w_flat = w_bf[:].rearrange("p q u e -> p (q u e)")
        first, second = query_halves
        nc.vector.quantize_mx(out=w_codes[:, first].bitcast(FP8X4), scales=w_plane[:, first], in_=w_flat[:, 0 : N // 2])
        nc.vector.quantize_mx(out=v_codes[:].bitcast(FP8X4), scales=v_plane[:], in_=v_bf[:])
        nc.vector.quantize_mx(out=w_codes[:, second].bitcast(FP8X4), scales=w_plane[:, second], in_=w_flat[:, N // 2 :])
        inv = sb.tile([P, 1], F32, name="inv", tag="turned", align_bytes=64)
        nc.vector.reciprocal(inv[:], total[:])

        y_ps = ps.tile([P, P], F32, name="y_ps")
        nc.tensor.matmul_mx(
            out=y_ps[:],
            lhsT=w_codes[:].bitcast(FP8X4),
            lhsT_scale=w_plane[:],
            rhs=v_codes[:].bitcast(FP8X4),
            rhs_scale=v_plane[:],
            start=True,
            stop=True,
        )
        y = sb.tile([P, P], F32, name="y", align_bytes=256)
        nc.vector.tensor_scalar(y[:], y_ps[:], inv[:], None, ALU.mult)
        nc.sync.dma_start(out[0], y[:])
